import numpy as np, ml_dtypes
CORES = [1,5,17,21,33,37,49,53]
N = 8
import mx_ref
BF = ml_dtypes.bfloat16
def pick(q, e):
    c = np.concatenate([q[0].reshape(128, -1, 4), np.zeros((128, 1, 4), np.uint8)], axis=1); s = np.concatenate([q[1], np.ones((16, 1), np.uint8)], axis=1)
    return (np.ascontiguousarray(c[:, e].reshape(128, -1)), np.ascontiguousarray(s[:, e]))
def join(*qs):
    return (np.concatenate([q[0] for q in qs], axis=1), np.concatenate([q[1] for q in qs], axis=1))
def put(q, e, v):
    c, s = q[0].reshape(128, -1, 4).copy(), q[1].copy(); c[:, e] = v[0].reshape(128, -1, 4); s[:, e] = v[1]
    return (c.reshape(128, -1), s)
def pk(c, s):
    return (np.ascontiguousarray(c), mx_ref.live(s))
def emit(q):
    return q[0], q[1]
def cut(t, i, w=512):
    return t[:, w * i:w * i + w]
def f(rng, *shape):
    return mx_ref.flush((rng.standard_normal(shape, dtype=np.float32) * np.exp2(rng.integers(-2, 3, shape[:-1] + (1,)))).astype(BF))
def wide(rng, *shape, cols=0):
    v = rng.standard_normal(shape, dtype=np.float32) * np.exp2(rng.integers(-12, 13, shape)).astype(np.float32)
    if cols: v *= np.repeat(np.exp2(rng.integers(-cols, cols + 1, shape[:-2] + (1, shape[-1] // 4))) * (rng.random(shape[:-2] + (1, shape[-1] // 4)) > 0.0625), 4, axis=-1).astype(np.float32)
    return mx_ref.flush(v.astype(BF))
P, R, O = 1024, 4, 2
C = P // 16
CLOUD = np.arange(N * P) % P // C
def same(t):
    return np.stack([t] * N)
def sizes(rng, *shape):
    return (1 + rng.random(shape, dtype=np.float32)) * (1 - 2 * rng.integers(0, 2, shape)).astype(np.float32)
def setup_inputs(rng):
    return {"x": f(rng, N, 128, 4 * P), "seed": same(f(rng, 128, 64)), "w": f(rng, N, 128, 512 * O)}
def setup_inputs_again(rng):
    d = setup_inputs(rng)
    half = rng.permutation(16) < 8
    four = rng.permutation(np.flatnonzero(half))[:4]
    huge, minus = np.isin(np.arange(16), four), np.isin(np.arange(16), four[:2])
    x, s = sizes(rng, N, 128, 4 * P), sizes(rng, 128, 64)
    x = np.where(np.repeat(half, 4 * C), np.abs(x), x)
    s = np.where(np.repeat(half, 4), np.abs(s), s)
    for b in np.flatnonzero(half):
        r, j = int(rng.integers(0, N)), int(b * C + rng.integers(0, C))
        if minus[b]: r, j = 0, int(b * C)
        x[r, :, 4 * j:4 * j + 4] *= np.float32(0.5 if huge[b] else 2.0 ** -8)
    by = np.where(huge, np.float32(2.0 ** 29), np.float32(1))
    x, s = x * np.repeat(by, 4 * C), s * np.repeat(np.where(minus, -by, by), 4)
    d["x"], d["seed"] = x.astype(BF), same(s.astype(BF))
    return d
def setup_inputs_late(rng):
    d = setup_inputs(rng)
    top = (np.arange(128) < 64)[:, None]
    a = np.stack([rng.permutation(C) < C // 2 for i in range(16 * N)]).reshape(N, 1, P)
    a = np.repeat(a, 4, axis=2)
    v = sizes(rng, N, 128, 4 * P)
    d["x"] = np.where(top, np.where(a, -np.abs(v), v * np.float32(2.0 ** -6)), np.where(a, 0, v)).astype(BF)
    d["seed"] = same(np.where(top, np.abs(sizes(rng, 128, 64)), 0).astype(BF))
    return d
def setup_inputs_one(rng):
    d = setup_inputs(rng)
    h = int(rng.integers(0, N))
    s = sizes(rng, 128, 64).astype(BF)
    d["seed"] = same(s)
    d["x"] = same(np.repeat(s.reshape(128, 16, 1, 4), C, axis=2).reshape(128, 4 * P))
    d["x"][h] = (sizes(rng, 128, 4 * P) * np.float32(2.0 ** -6)).astype(BF)
    return d
def setup_inputs_spread(rng):
    d = setup_inputs(rng)
    x, s = wide(rng, N, 128, 4 * P, cols=6).astype(np.float32), wide(rng, 128, 64).astype(np.float32)
    plus = rng.permutation(16) < 4
    x = np.where(np.repeat(plus, 4 * C), np.abs(x), x)
    s = np.where(np.repeat(plus, 4), np.abs(s), s)
    for b in np.flatnonzero(plus):
        for r, zero in zip(np.sort(rng.permutation(N)[:2]), (0.0, -0.0)):
            j = int(b * C + rng.integers(0, C))
            x[r, :, 4 * j:4 * j + 4] = np.float32(zero)
    d["x"], d["seed"] = x.astype(BF), same(s.astype(BF))
    return d
def setup_inputs_ties(rng):
    d = setup_inputs(rng)
    v = rng.standard_normal((128, 16, 12, 4), dtype=np.float32)
    v[:64, 1::2, 1::2] = v[:64, 1::2, ::2]
    s = rng.standard_normal((128, 16, 4), dtype=np.float32)
    s[64:, 1::2] = 0
    x = np.zeros((N, 128, 16, C, 4), np.float32)
    for b in range(16):
        own = np.stack([rng.permutation(N) < N // 2 for i in range(12)])
        own[1] = ~own[0]
        for r in range(N):
            e = rng.permutation(np.resize(np.flatnonzero(own[:, r]), C))
            x[r][:, b] = v[:, b][:, e]
    d["x"] = mx_ref.flush(x.reshape(N, 128, 4 * P).astype(BF))
    d["seed"] = same(mx_ref.flush(s.reshape(128, 64).astype(BF)))
    return d
def check_inputs(d):
    b = []
    for k in ("x", "seed", "w"):
        v = np.abs(d[k].astype(np.float32))
        if not (np.isfinite(v).all() and ((v == 0) | (v >= 2.0 ** -30) & (v <= 2.0 ** 30)).all()): b.append("a value of " + k)
    s = d["seed"].astype(np.float32)
    if not (s == s[:1]).all(): b.append("seed isn't the same on all ranks")
    return b
def reference(x, seed, w):
    q = [mx_ref.quantize(np.ascontiguousarray(x[r])) for r in range(N)]
    every = join(*q)
    c = mx_ref.quantize(np.ascontiguousarray(seed[0]))
    won, nb = [], np.zeros((R, 16), np.float32)
    for t in range(R):
        k = pick(c, np.concatenate([np.arange(16), np.full(112, -1)]))
        s = np.concatenate([mx_ref.matmul(k, v)[:16] for v in q], axis=1)
        s = s[CLOUD, np.arange(N * P)] + np.float32(0)
        m = s if t == 0 else np.maximum(m, s)
        e = []
        for b in range(16):
            i = np.flatnonzero(CLOUD == b)
            e.append(int(i[np.argmin(m[i])]))
        c = pick(every, np.array(e))
        won.append(c)
        nb[t] = e
    u = join(*won)
    oc, osc = emit(u)
    y = np.stack([np.concatenate([mx_ref.matmul(mx_ref.quantize(np.ascontiguousarray(cut(w[r], o))), u) for o in range(O)], axis=1) for r in range(N)])
    return {"oc": same(oc), "osc": same(osc), "nb": same(nb), "y": y}

@@ -1,0 +1,382 @@
+from concourse.bass import DstId, RemoteDMATransfer
+from concourse.mybir import dt, AluOpType, AxisListType, ActivationFunctionType
+
+R, P, O = 4, 1024, 2
+F8 = "float8_e4m3fn_x4"
+SCRATCH = {
+    "xb": ("sbuf", [128, 4 * P], "bfloat16"),
+    "wb": ("sbuf", [128, 512 * O], "bfloat16"),
+    "sd": ("sbuf", [128, 576], "bfloat16"),
+    "wq": ("sbuf", [128, 128 * O], F8), "wp": ("sbuf", [128, 128 * O], "uint8"),
+    "ip": ("sbuf", [128, 8], "int32"),
+    "q32": ("sbuf", [128, 32], "float32"),
+    "j4": ("sbuf", [128, 256], "float32"),
+    "c4": ("sbuf", [128, 4], "float32"),
+    "cf": ("sbuf", [128, 16], "float32"),
+    "cl": ("sbuf", [128, 32], "uint16"),
+    "d1": ("sbuf", [128, 264], "bfloat16"),
+    "d0": ("sbuf", [128, 264], "bfloat16"),
+    "sc": ("sbuf", [128, 264], "bfloat16"),
+    "tmp": ("sbuf", [128, 256], "float32"),
+    "ofs": ("sbuf", [128, 32], "uint16"),
+    "nl": ("sbuf", [128, 16], "float32"),
+    "res": ("sbuf", [128, 4], "float32"),
+    "resl": ("sbuf", [128, 4], "float32"),
+    "nbv": ("sbuf", [128, 4], "float32"),
+    "ysb": ("sbuf", [128, 64 * O], "float32"),
+    "ps": ("psum", [128, 512], "float32"),
+}
+for _t in range(R + 1):
+    SCRATCH["xq%d" % _t] = ("sbuf", [128, P + 16], F8)
+    SCRATCH["xp%d" % _t] = ("sbuf", [128, P + 16], "uint8")
+    SCRATCH["dq%d" % _t] = ("sbuf", [128, 144], F8)
+    SCRATCH["dp%d" % _t] = ("sbuf", [128, 144], "uint8")
+    SCRATCH["mk%d" % _t] = ("sbuf", [128, 264], "float32")
+    if _t:
+        SCRATCH["wc%d" % _t] = ("sbuf", [128, 512], F8)
+        SCRATCH["ws%d" % _t] = ("sbuf", [128, 512], "uint8")
+        SCRATCH["pq%d" % _t] = ("sbuf", [128, 16], F8)
+        SCRATCH["pp%d" % _t] = ("sbuf", [128, 16], "uint8")
+        SCRATCH["mq%d" % _t] = ("sbuf", [128, 64], F8)
+        SCRATCH["mp%d" % _t] = ("sbuf", [128, 64], "uint8")
+        SCRATCH["qm%d" % _t] = ("sbuf", [128, 16], "float32")
+        SCRATCH["ym%d" % _t] = ("sbuf", [128, 4], "float32")
+        SCRATCH["yn%d" % _t] = ("sbuf", [128, 4], "float32")
+for _k in range(6):
+    SCRATCH["py%d" % _k] = ("psum", [128, 512], "float32")
+SEMAPHORES = ["v", "s", "t", "ty", "iot", "ls", "ld_s", "ld_w", "st", "sty", "qn", "rs"]
+SEMAPHORES += ["ld%d" % q for q in range(4)] + ["wc%d" % q for q in range(4)] + ["ws%d" % q for q in range(4)]
+SEMAPHORES += [n + "%d" % t for t in range(1, R + 1) for n in ("ym", "yn", "yc", "ys", "qm", "qc", "qs", "dc", "ds")]
+
+BIG = 4096.0
+FAR = 1e29
+
+
+def rank_program(g, core, T, topo):
+    rank = T.rank_of(core)
+    if rank is None:
+        return
+    A = AluOpType
+    X = AxisListType.X
+    CP = ActivationFunctionType.Copy
+    S = T.sem
+    chips, ranks_of = [], {}
+    for c in T.cores:
+        if topo.chip(c) not in ranks_of:
+            chips.append(topo.chip(c))
+            ranks_of[topo.chip(c)] = []
+        ranks_of[topo.chip(c)].append(c)
+    me = chips.index(topo.chip(core))
+    ab = ranks_of[chips[me]].index(core)
+    mate = ranks_of[chips[me]][1 - ab]
+    nch = len(chips)
+    peers = [ranks_of[chips[(me + k) % nch]][ab] for k in range(1, nch)]
+
+    cnt = {"v": 0, "vw": 0, "s": 0, "sw": 0, "ty": 0, "ls": 0, "st": 0}
+
+    def V(call):
+        if cnt["vw"] < cnt["v"]:
+            g.vector.wait_ge(S.v, cnt["v"])
+            cnt["vw"] = cnt["v"]
+        call().then_inc(S.v, 1)
+        cnt["v"] += 1
+        return cnt["v"]
+
+    def AC(call):
+        if cnt["sw"] < cnt["s"]:
+            g.scalar.wait_ge(S.s, cnt["s"])
+            cnt["sw"] = cnt["s"]
+        call().then_inc(S.s, 1)
+        cnt["s"] += 1
+        return cnt["s"]
+
+    def bits(es):
+        return sum(1 << e for e in es)
+
+    def dst(c):
+        a = topo.addr(c)
+        return DstId(rid=a[0], pnc=a[1])
+
+    def to_mate(out, in_, sem):
+        rid, pid = topo.addr(mate)[:2]
+        es = topo.engines(core, mate)[:8]
+        g.remote_dma(out, in_, sem, S.ls, pid, rid, bits(es))
+        cnt["ls"] += len(es)
+
+    MATE_INC = 8
+    PEER_INC = 8
+
+    def to_peers(out, in_, sem, turn):
+        es = topo.engines(core, peers[0])[:8]
+        cut = [es[0:4], es[4:6], es[6:8]] if turn == 0 else [es[4:8], es[0:2], es[2:4]]
+        g.remote_dma_fused([RemoteDMATransfer(dst_ids=[dst(c)], dma_engine_mask=bits(e), remote_sem=sem, src=in_, dst=out)
+                            for c, e in zip(peers, cut)], local_sem=S.ls)
+        cnt["ls"] += sum(len(e) for e in cut)
+
+    def u8(ap):
+        return ap.bitcast(dt.uint8)
+
+    def u32(ap):
+        return ap.bitcast(dt.uint32)
+
+    tcol = [0]
+
+    def tmp(n=1):
+        a = tcol[0]
+        tcol[0] += n
+        return T.tmp[:, a:a + n]
+
+    vec = g.vector
+    g.sync.dma_start(T.sd[:, 512:576], T.seed[:]).then_inc(S.ld_s, 16)
+    for q in (0, 2):
+        g.sync.dma_start(T.xb[:, 1024 * q:1024 * q + 1024], T.x[:, 1024 * q:1024 * q + 1024]).then_inc(S["ld%d" % q], 16)
+    for q in (1, 3):
+        g.scalar.dma_start(T.xb[:, 1024 * q:1024 * q + 1024], T.x[:, 1024 * q:1024 * q + 1024]).then_inc(S["ld%d" % q], 16)
+    g.sync.dma_start(T.wb[:], T.w[:]).then_inc(S.ld_w, 16)
+
+    g.iota(T.ip[:, 0:1], [[0, 1]], 0, 1).then_inc(S.iot, 1)
+    g.iota(T.q32[:], [[1, 4], [0, 8]], 0, 0, allow_small_or_imprecise_dtypes=True).then_inc(S.iot, 1)
+    g.iota(T.j4[:], [[1, 4], [0, 64]], 0, 0, allow_small_or_imprecise_dtypes=True).then_inc(S.iot, 1)
+    g.iota(T.c4[:], [[1, 4]], -4, 0, allow_small_or_imprecise_dtypes=True).then_inc(S.iot, 1)
+
+    def cf(k):
+        return T.cf[:, k:k + 1]
+
+    V(lambda: vec.memset(T.sd[:, 0:512], 0.0))
+    V(lambda: vec.memset(T.d1[:], -1.0))
+    V(lambda: vec.memset(T.d1[:, 3:4], -256.0))
+    V(lambda: vec.memset(T.d1[:, 260:261], 0.0))
+    vec.wait_ge(S.iot, 4)
+    V(lambda: vec.tensor_scalar(T.ip[:, 1:2], T.ip[:, 0:1], 15, None, A.bitwise_and))
+    V(lambda: vec.tensor_scalar(T.ip[:, 2:3], T.ip[:, 1:2], 2, None, A.logical_shift_right))
+    V(lambda: vec.tensor_scalar(T.ip[:, 3:4], T.ip[:, 0:1], 3, None, A.bitwise_and))
+    V(lambda: vec.tensor_scalar(T.ip[:, 4:5], T.ip[:, 0:1], 4, None, A.logical_shift_right))
+    V(lambda: vec.tensor_copy(T.cf[:, 0:4], T.ip[:, 1:5]))
+    fb, fq, fr, fg = cf(0), cf(1), cf(2), cf(3)
+    b128, b64, base, bnum, dX = cf(4), cf(5), cf(6), cf(7), cf(8)
+    V(lambda: vec.tensor_scalar(b128, fb, 128.0, None, A.add))
+    V(lambda: vec.tensor_scalar(T.cl[:], T.q32[:], fq, b128, A.is_equal, A.mult))
+    vec.wait_ge(S.ld_s, 16)
+    d0_done = V(lambda: vec.quantize_mx(T.dq0[:, 0:144], T.dp0[:, 0:144], T.sd[:, 0:576]))
+
+    def windows(t):
+        q0, p0, wc, ws = T["dq%d" % (t - 1)], T["dp%d" % (t - 1)], T["wc%d" % t], T["ws%d" % t]
+        for q in range(4):
+            vec.tensor_copy(u32(wc[:, 128 * q:128 * q + 128]), u32(q0[:, 0:144]).indirect(T.cl[:, 8 * q:8 * q + 8])).then_inc(S["wc%d" % q], 1)
+            g.scalar.activation(ws[:, 128 * q:128 * q + 128], p0[:, 0:144].indirect(T.cl[:, 8 * q:8 * q + 8]), CP).then_inc(S["ws%d" % q], 1)
+
+    vec.wait_ge(S.v, d0_done)
+    cnt["vw"] = cnt["v"]
+    g.scalar.wait_ge(S.v, d0_done)
+    windows(1)
+    V(lambda: vec.tensor_scalar(T.tmp[:, 0:256], T.j4[:], fr, 2 * FAR, A.not_equal, A.mult))
+    V(lambda: vec.tensor_scalar(T.mk0[:, 4:260], T.tmp[:, 0:256], -FAR, None, A.add))
+    V(lambda: vec.tensor_scalar(b64, fb, 64.0, None, A.add))
+    V(lambda: vec.tensor_scalar(base, fq, 256.0, 256.0, A.mult, A.add))
+    V(lambda: vec.tensor_scalar(bnum, base, float(P * rank), None, A.add))
+    V(lambda: vec.tensor_scalar(dX, fq, -256.0, fb, A.mult, A.add))
+    V(lambda: vec.tensor_scalar(dX, dX, 768.0 if ab == 0 else 1280.0, None, A.add))
+    for t in range(1, R + 1):
+        if (t - 1) % 2 == ab:
+            V(lambda: vec.tensor_scalar(cf(8 + t), fg, float(t - 1), None, A.is_equal))
+    for t in range(1, R + 1):
+        V(lambda: vec.quantize_mx(T["dq%d" % t][:, 0:128], T["dp%d" % t][:, 0:128], T.sd[:, 0:512]))
+
+    def quant_x(k, q):
+        return V(lambda: vec.quantize_mx(T["xq%d" % k][:, 256 * q:256 * q + 256], T["xp%d" % k][:, 256 * q:256 * q + 256],
+                                         T.xb[:, 1024 * q:1024 * q + 1024]))
+
+    mine = 1 if ab == 0 else 0
+    xdone = []
+    for q in range(4):
+        vec.wait_ge(S["ld%d" % q], 16)
+        xdone.append(quant_x(mine, q))
+    xq, xp = T["xq%d" % mine], T["xp%d" % mine]
+
+    def score(t):
+        for q in range(4):
+            if t == 1:
+                g.tensor.wait_ge(S.v, xdone[q])
+            g.tensor.wait_ge(S["wc%d" % q], t)
+            g.tensor.wait_ge(S["ws%d" % q], t)
+            i = g.tensor.matmul_mx(T.ps[:, 0:256], T["wc%d" % t][:, 128 * q:128 * q + 128], T["ws%d" % t][:, 128 * q:128 * q + 128],
+                                   xq[:, 256 * q:256 * q + 256], xp[:, 256 * q:256 * q + 256], q == 0, q == 3)
+        i.then_inc(S.t, 1)
+
+    def source(t, root):
+        k = t if root else t - 1
+        return T["xq%d" % k], T["xp%d" % k]
+
+    ydone, wdone = {}, [0]
+
+    def products(t):
+        k = 2 * ((t - 1) % 3)
+        if t == 1:
+            g.tensor.wait_ge(S.v, wdone[0])
+        if t == 4:
+            g.tensor.wait_ge(S.s, ydone[1])
+        for o in range(O):
+            g.tensor.matmul_mx(T["py%d" % (k + o)][:, 0:128], T.wq[:, 128 * o:128 * o + 128], T.wp[:, 128 * o:128 * o + 128],
+                               T["dq%d" % t][:, 16:144], T["dp%d" % t][:, 16:144], True, True).then_inc(S.ty, 1)
+            cnt["ty"] += 1
+        g.scalar.wait_ge(S.ty, cnt["ty"])
+        for o in range(O):
+            ydone[t] = AC(lambda: g.scalar.activation(T.ysb[:, 64 * o + 16 * (t - 1):64 * o + 16 * t],
+                                                      T["py%d" % (k + o)][:, 112:128], CP))
+
+    oh_acc, num_acc = [], []
+
+    def resolve():
+        pr = tmp(4)
+        vec.wait_ge(S.qn, PEER_INC)
+        V(lambda: vec.tensor_tensor(pr, oh_acc[0], T.nl[:, 0:16:4], A.mult))
+        v = V(lambda: vec.tensor_reduce(T.res[:, 0:1], pr, X, A.add))
+        g.wait_ge(S.v, v)
+        to_mate(T.resl[:, 0:1], T.res[:, 0:1], S.rs)
+
+    for t in range(1, R + 1):
+        root = (t - 1) % 2 == ab
+        n = "%d" % t
+        mk, qm, ym = T["mk" + n], T["qm" + n], T["ym" + n]
+        score(t)
+        if t > 1:
+            products(t - 1)
+        vec.wait_ge(S.t, t)
+        V(lambda: vec.tensor_tensor(mk[:, 4:260], T["mk%d" % (t - 1)][:, 4:260], T.ps[:, 0:256], A.max))
+        if root:
+            lo, hi = (4, 261) if ab == 0 else (3, 260)
+            vec.wait_ge(S["ym" + n], MATE_INC)
+            low = qm[:, 4 * me:4 * me + 1]
+        else:
+            lo, hi = 4, 260
+            low = ym[:, 0:1]
+        vm = V(lambda: vec.tensor_reduce(low, mk[:, lo:hi], X, A.min))
+        g.wait_ge(S.v, vm)
+        if root:
+            to_peers(low, low, S["qm" + n], 0)
+        else:
+            c = 260 if ab == 1 else 3
+            to_mate(mk[:, c:c + 1], low, S["ym" + n])
+        V(lambda: vec.tensor_scalar(T.d0[:, lo:hi], mk[:, lo:hi], low, BIG, A.is_gt, A.mult))
+        V(lambda: vec.tensor_tensor_scan(T.sc[:, lo:hi], T.d0[:, lo:hi], T.d1[:, lo:hi], BIG, A.min, A.add))
+        last = T.sc[:, hi - 1:hi]
+        off = T.ofs[:, 4 * t:4 * t + 1]
+        sq, sp = source(t, root)
+        if root:
+            e = tmp()
+            lim, cmp = (-0.5, A.is_gt) if ab == 0 else (-300.0, A.is_lt)
+            V(lambda: vec.tensor_scalar(e, last, lim, dX, cmp, A.mult))
+            vo = V(lambda: vec.tensor_scalar(off, last, base, e, A.add, A.add))
+            oq, op, wid = T["mq" + n][:, 16 * me:16 * me + 16], T["mp" + n][:, 16 * me:16 * me + 16], P + 16
+            vec.wait_ge(S["yc" + n], MATE_INC)
+            g.scalar.wait_ge(S["ys" + n], MATE_INC)
+        else:
+            vo = V(lambda: vec.tensor_scalar(off, last, base, None, A.add))
+            oq, op, wid = T["pq" + n][:, 0:16], T["pp" + n][:, 0:16], P
+        vp = V(lambda: vec.tensor_copy(u32(oq), u32(sq[:, 0:wid]).indirect(off)))
+        g.scalar.wait_ge(S.v, vo)
+        sp_ = AC(lambda: g.scalar.activation(op, sp[:, 0:wid].indirect(off), CP))
+        g.wait_ge(S.v, vp)
+        if root:
+            to_peers(u8(oq), u8(oq), S["qc" + n], 0)
+            g.wait_ge(S.s, sp_)
+            to_peers(op, op, S["qs" + n], 1)
+        else:
+            to_mate(u8(T["xq" + n][:, P:P + 16]), u8(oq), S["yc" + n])
+            g.wait_ge(S.s, sp_)
+            to_mate(T["xp" + n][:, P:P + 16], op, S["ys" + n])
+        if root:
+            own, fl, df, num = tmp(), tmp(), tmp(), tmp()
+            V(lambda: vec.tensor_scalar(own, last, bnum, None, A.add))
+            V(lambda: vec.tensor_scalar(fl, last, lim, None, cmp))
+            vec.wait_ge(S["yn" + n], MATE_INC)
+            V(lambda: vec.tensor_tensor(df, T["yn" + n][:, 0:1], own, A.subtract))
+            V(lambda: vec.tensor_scalar(num, df, fl, own, A.mult, A.add))
+            if not num_acc:
+                num_acc.append(tmp())
+                V(lambda: vec.tensor_scalar(num_acc[0], num, cf(8 + t), None, A.mult))
+            else:
+                nl = T.nl[:, 4 * me:4 * me + 1]
+                vn = V(lambda: vec.tensor_scalar(nl, num, cf(8 + t), num_acc[0], A.mult, A.add))
+                g.wait_ge(S.v, vn)
+                to_peers(nl, nl, S.qn, 0)
+        else:
+            vn = V(lambda: vec.tensor_scalar(ym[:, 1:2], last, bnum, None, A.add))
+            g.wait_ge(S.v, vn)
+            to_mate(T["yn" + n][:, 0:1], ym[:, 1:2], S["yn" + n])
+        if t == 1:
+            vec.wait_ge(S.ld_w, 16)
+            wdone[0] = V(lambda: vec.quantize_mx(T.wq[:, 0:128 * O], T.wp[:, 0:128 * O], T.wb[:, 0:512 * O]))
+            for k in ((3,) if ab == 0 else (2, 4)):
+                for q in range(4):
+                    quant_x(k, q)
+        if t == R and not root:
+            resolve()
+        dq, dp = T["dq" + n], T["dp" + n]
+        if root:
+            rm, d4, s4 = tmp(), tmp(4), tmp(4)
+            vec.wait_ge(S["qm" + n], PEER_INC)
+            V(lambda: vec.tensor_reduce(rm, qm[:, 0:16:4], X, A.min))
+            V(lambda: vec.tensor_scalar(d4, qm[:, 0:16:4], rm, BIG, A.is_gt, A.mult))
+            V(lambda: vec.tensor_tensor_scan(s4, d4, T.d1[:, 4:8], BIG, A.min, A.add))
+            i4 = T.tmp[:, tcol[0] - 1:tcol[0]]
+            off2 = T.ofs[:, 4 * t + 2:4 * t + 3]
+            vo = V(lambda: vec.tensor_scalar(off2, i4, 16.0, b64, A.mult, A.add))
+            vec.wait_ge(S["qc" + n], PEER_INC)
+            g.scalar.wait_ge(S["qs" + n], PEER_INC)
+            vp = V(lambda: vec.tensor_copy(u32(dq[:, 128:144]), u32(T["mq" + n][:, 0:64]).indirect(off2)))
+            g.scalar.wait_ge(S.v, vo)
+            sp_ = AC(lambda: g.scalar.activation(dp[:, 128:144], T["mp" + n][:, 0:64].indirect(off2), CP))
+            g.wait_ge(S.v, vp)
+            to_mate(u8(dq[:, 128:144]), u8(dq[:, 128:144]), S["dc" + n])
+            g.wait_ge(S.s, sp_)
+            to_mate(dp[:, 128:144], dp[:, 128:144], S["ds" + n])
+            vec.wait_ge(S.v, vp)
+            cnt["vw"] = cnt["v"]
+            g.scalar.wait_ge(S.s, sp_)
+            cnt["sw"] = cnt["s"]
+            g.sync.wait_ge(S.v, vp)
+            g.sync.wait_ge(S.s, sp_)
+            if t == R:
+                g.tensor.wait_ge(S.v, vp)
+                g.tensor.wait_ge(S.s, sp_)
+        else:
+            if t < R:
+                vec.wait_ge(S["dc" + n], MATE_INC)
+                g.scalar.wait_ge(S["ds" + n], MATE_INC)
+            else:
+                g.tensor.wait_ge(S["dc" + n], MATE_INC)
+                g.tensor.wait_ge(S["ds" + n], MATE_INC)
+            g.sync.wait_ge(S["dc" + n], MATE_INC)
+            g.sync.wait_ge(S["ds" + n], MATE_INC)
+        if t < R:
+            windows(t + 1)
+        g.sync.dma_start(T.oc[:, 64 * (t - 1):64 * t], u8(dq[:, 128:144])).then_inc(S.st, 16)
+        for k in range(4):
+            g.sync.dma_start(T.osc[4 * k:4 * k + 4, 16 * (t - 1):16 * t], dp[32 * k:32 * k + 4, 128:144]).then_inc(S.st, 16)
+        cnt["st"] += 80
+        if root:
+            oh = tmp(4)
+            V(lambda: vec.tensor_scalar(oh, T.c4[:], i4, cf(8 + t), A.is_equal, A.mult))
+            if not oh_acc:
+                oh_acc.append(oh)
+            else:
+                oh2 = tmp(4)
+                V(lambda: vec.tensor_tensor(oh2, oh, oh_acc[0], A.add))
+                oh_acc[0] = oh2
+        if t == R:
+            products(R)
+            g.scalar.wait_ge(S.s, cnt["s"])
+            g.scalar.dma_start(T.y[:], T.ysb[:]).then_inc(S.sty, 16)
+            if root:
+                resolve()
+    vec.wait_ge(S.rs, MATE_INC)
+    vnb = V(lambda: vec.tensor_tensor(T.nbv[:, 0:1], T.res[:, 0:1], T.resl[:, 0:1], A.add))
+    g.sync.wait_ge(S.v, vnb)
+    g.sync.dma_start(T.nb[:], T.nbv[0:64, 0:1]).then_inc(S.st, 16)
+    cnt["st"] += 16
+    g.sync.wait_ge(S.st, cnt["st"])
+    g.scalar.wait_ge(S.sty, 16)
+    g.wait_ge(S.ls, cnt["ls"])
+    g.wait_ge(S.v, cnt["v"])
+    g.wait_ge(S.s, cnt["s"])

@@ -1,7 +1,7 @@
 from concourse.bass import DstId, RemoteDMATransfer
 from concourse.mybir import dt, AluOpType, AxisListType, ActivationFunctionType
 
-R, P, O = 4, 1024, 2
+R, P, O, N = 4, 1024, 2, 8
 F8 = "float8_e4m3fn_x4"
 SCRATCH = {
     "xb": ("sbuf", [128, 4 * P], "bfloat16"),
@@ -12,6 +12,7 @@ SCRATCH = {
     "q32": ("sbuf", [128, 32], "float32"),
     "j4": ("sbuf", [128, 256], "float32"),
     "c4": ("sbuf", [128, 4], "float32"),
+    "c8": ("sbuf", [128, 4], "float32"),
     "cf": ("sbuf", [128, 16], "float32"),
     "cl": ("sbuf", [128, 32], "uint16"),
     "d1": ("sbuf", [128, 264], "bfloat16"),
@@ -19,7 +20,7 @@ SCRATCH = {
     "sc": ("sbuf", [128, 264], "bfloat16"),
     "tmp": ("sbuf", [128, 256], "float32"),
     "ofs": ("sbuf", [128, 32], "uint16"),
-    "nl": ("sbuf", [128, 16], "float32"),
+    "nl": ("sbuf", [128, 32], "uint16"),
     "res": ("sbuf", [128, 4], "float32"),
     "resl": ("sbuf", [128, 4], "float32"),
     "nbv": ("sbuf", [128, 4], "float32"),
@@ -33,18 +34,19 @@ for _t in range(R + 1):
     SCRATCH["dp%d" % _t] = ("sbuf", [128, 144], "uint8")
     SCRATCH["mk%d" % _t] = ("sbuf", [128, 264], "float32")
     if _t:
+        _m = N if _t == 1 else N // 2
         SCRATCH["wc%d" % _t] = ("sbuf", [128, 512], F8)
         SCRATCH["ws%d" % _t] = ("sbuf", [128, 512], "uint8")
         SCRATCH["pq%d" % _t] = ("sbuf", [128, 16], F8)
         SCRATCH["pp%d" % _t] = ("sbuf", [128, 16], "uint8")
-        SCRATCH["mq%d" % _t] = ("sbuf", [128, 64], F8)
-        SCRATCH["mp%d" % _t] = ("sbuf", [128, 64], "uint8")
-        SCRATCH["qm%d" % _t] = ("sbuf", [128, 16], "float32")
+        SCRATCH["mq%d" % _t] = ("sbuf", [128, 16 * _m], F8)
+        SCRATCH["mp%d" % _t] = ("sbuf", [128, 16 * _m], "uint8")
+        SCRATCH["qm%d" % _t] = ("sbuf", [128, 4 * _m], "float32")
         SCRATCH["ym%d" % _t] = ("sbuf", [128, 4], "float32")
         SCRATCH["yn%d" % _t] = ("sbuf", [128, 4], "float32")
 for _k in range(6):
     SCRATCH["py%d" % _k] = ("psum", [128, 512], "float32")
-SEMAPHORES = ["v", "s", "t", "ty", "iot", "ls", "ld_s", "ld_w", "st", "sty", "qn", "rs"]
+SEMAPHORES = ["v", "s", "t", "ty", "iot", "iou", "ls", "ld_s", "ld_w", "st", "sty", "qn", "rs"]
 SEMAPHORES += ["ld%d" % q for q in range(4)] + ["wc%d" % q for q in range(4)] + ["ws%d" % q for q in range(4)]
 SEMAPHORES += [n + "%d" % t for t in range(1, R + 1) for n in ("ym", "yn", "yc", "ys", "qm", "qc", "qs", "dc", "ds")]
 
@@ -70,7 +72,8 @@ def rank_program(g, core, T, topo):
     ab = ranks_of[chips[me]].index(core)
     mate = ranks_of[chips[me]][1 - ab]
     nch = len(chips)
-    peers = [ranks_of[chips[(me + k) % nch]][ab] for k in range(1, nch)]
+    others = [chips[(me + k) % nch] for k in range(1, nch)]
+    peers = [ranks_of[h][ab] for h in others]
 
     cnt = {"v": 0, "vw": 0, "s": 0, "sw": 0, "ty": 0, "ls": 0, "st": 0}
 
@@ -97,21 +100,32 @@ def rank_program(g, core, T, topo):
         a = topo.addr(c)
         return DstId(rid=a[0], pnc=a[1])
 
+    ES = topo.engines(core, peers[0])[:8]
+
     def to_mate(out, in_, sem):
         rid, pid = topo.addr(mate)[:2]
-        es = topo.engines(core, mate)[:8]
-        g.remote_dma(out, in_, sem, S.ls, pid, rid, bits(es))
-        cnt["ls"] += len(es)
+        g.remote_dma(out, in_, sem, S.ls, pid, rid, bits(ES))
+        cnt["ls"] += len(ES)
+
+    def fused(parts):
+        g.remote_dma_fused([RemoteDMATransfer(dst_ids=[dst(c)], dma_engine_mask=bits(e), remote_sem=sem, src=in_, dst=out)
+                            for c, e, out, in_, sem in parts], local_sem=S.ls)
+        cnt["ls"] += sum(len(p[1]) for p in parts)
 
     MATE_INC = 8
     PEER_INC = 8
+    FLAT_INC = 16
 
     def to_peers(out, in_, sem, turn):
-        es = topo.engines(core, peers[0])[:8]
-        cut = [es[0:4], es[4:6], es[6:8]] if turn == 0 else [es[4:8], es[0:2], es[2:4]]
-        g.remote_dma_fused([RemoteDMATransfer(dst_ids=[dst(c)], dma_engine_mask=bits(e), remote_sem=sem, src=in_, dst=out)
-                            for c, e in zip(peers, cut)], local_sem=S.ls)
-        cnt["ls"] += sum(len(e) for e in cut)
+        cut = [ES[0:4], ES[4:6], ES[6:8]] if turn == 0 else [ES[4:8], ES[0:2], ES[2:4]]
+        fused([(c, e, out, in_, sem) for c, e in zip(peers, cut)])
+
+    def to_roots(out, in_, sem, turn):
+        if ab == 0:
+            to_peers(out, in_, sem, turn)
+        else:
+            to = [ranks_of[h][0] for h in others] + [mate]
+            fused([(c, ES[2 * k:2 * k + 2], out, in_, sem) for k, c in enumerate(to)])
 
     def u8(ap):
         return ap.bitcast(dt.uint8)
@@ -132,21 +146,23 @@ def rank_program(g, core, T, topo):
         g.sync.dma_start(T.xb[:, 1024 * q:1024 * q + 1024], T.x[:, 1024 * q:1024 * q + 1024]).then_inc(S["ld%d" % q], 16)
     for q in (1, 3):
         g.scalar.dma_start(T.xb[:, 1024 * q:1024 * q + 1024], T.x[:, 1024 * q:1024 * q + 1024]).then_inc(S["ld%d" % q], 16)
+    g.sync.wait_ge(S.ld3, 16)
     g.sync.dma_start(T.wb[:], T.w[:]).then_inc(S.ld_w, 16)
 
     g.iota(T.ip[:, 0:1], [[0, 1]], 0, 1).then_inc(S.iot, 1)
     g.iota(T.q32[:], [[1, 4], [0, 8]], 0, 0, allow_small_or_imprecise_dtypes=True).then_inc(S.iot, 1)
-    g.iota(T.j4[:], [[1, 4], [0, 64]], 0, 0, allow_small_or_imprecise_dtypes=True).then_inc(S.iot, 1)
-    g.iota(T.c4[:], [[1, 4]], -4, 0, allow_small_or_imprecise_dtypes=True).then_inc(S.iot, 1)
+    g.iota(T.j4[:], [[1, 4], [0, 64]], 0, 0, allow_small_or_imprecise_dtypes=True).then_inc(S.iou, 1)
+    g.iota(T.c4[:], [[1, 4]], -4, 0, allow_small_or_imprecise_dtypes=True).then_inc(S.iou, 1)
+    g.iota(T.c8[:], [[2, 4]], -8, 0, allow_small_or_imprecise_dtypes=True).then_inc(S.iou, 1)
 
     def cf(k):
         return T.cf[:, k:k + 1]
 
+    def zeros(t):
+        V(lambda: vec.quantize_mx(T["dq%d" % t][:, 0:128], T["dp%d" % t][:, 0:128], T.sd[:, 0:512]))
+
     V(lambda: vec.memset(T.sd[:, 0:512], 0.0))
-    V(lambda: vec.memset(T.d1[:], -1.0))
-    V(lambda: vec.memset(T.d1[:, 3:4], -256.0))
-    V(lambda: vec.memset(T.d1[:, 260:261], 0.0))
-    vec.wait_ge(S.iot, 4)
+    vec.wait_ge(S.iot, 2)
     V(lambda: vec.tensor_scalar(T.ip[:, 1:2], T.ip[:, 0:1], 15, None, A.bitwise_and))
     V(lambda: vec.tensor_scalar(T.ip[:, 2:3], T.ip[:, 1:2], 2, None, A.logical_shift_right))
     V(lambda: vec.tensor_scalar(T.ip[:, 3:4], T.ip[:, 0:1], 3, None, A.bitwise_and))
@@ -156,6 +172,7 @@ def rank_program(g, core, T, topo):
     b128, b64, base, bnum, dX = cf(4), cf(5), cf(6), cf(7), cf(8)
     V(lambda: vec.tensor_scalar(b128, fb, 128.0, None, A.add))
     V(lambda: vec.tensor_scalar(T.cl[:], T.q32[:], fq, b128, A.is_equal, A.mult))
+    zeros(1)
     vec.wait_ge(S.ld_s, 16)
     d0_done = V(lambda: vec.quantize_mx(T.dq0[:, 0:144], T.dp0[:, 0:144], T.sd[:, 0:576]))
 
@@ -169,29 +186,24 @@ def rank_program(g, core, T, topo):
     cnt["vw"] = cnt["v"]
     g.scalar.wait_ge(S.v, d0_done)
     windows(1)
-    V(lambda: vec.tensor_scalar(T.tmp[:, 0:256], T.j4[:], fr, 2 * FAR, A.not_equal, A.mult))
-    V(lambda: vec.tensor_scalar(T.mk0[:, 4:260], T.tmp[:, 0:256], -FAR, None, A.add))
-    V(lambda: vec.tensor_scalar(b64, fb, 64.0, None, A.add))
-    V(lambda: vec.tensor_scalar(base, fq, 256.0, 256.0, A.mult, A.add))
-    V(lambda: vec.tensor_scalar(bnum, base, float(P * rank), None, A.add))
-    V(lambda: vec.tensor_scalar(dX, fq, -256.0, fb, A.mult, A.add))
-    V(lambda: vec.tensor_scalar(dX, dX, 768.0 if ab == 0 else 1280.0, None, A.add))
-    for t in range(1, R + 1):
-        if (t - 1) % 2 == ab:
-            V(lambda: vec.tensor_scalar(cf(8 + t), fg, float(t - 1), None, A.is_equal))
-    for t in range(1, R + 1):
-        V(lambda: vec.quantize_mx(T["dq%d" % t][:, 0:128], T["dp%d" % t][:, 0:128], T.sd[:, 0:512]))
 
     def quant_x(k, q):
         return V(lambda: vec.quantize_mx(T["xq%d" % k][:, 256 * q:256 * q + 256], T["xp%d" % k][:, 256 * q:256 * q + 256],
                                          T.xb[:, 1024 * q:1024 * q + 1024]))
 
-    mine = 1 if ab == 0 else 0
     xdone = []
     for q in range(4):
         vec.wait_ge(S["ld%d" % q], 16)
-        xdone.append(quant_x(mine, q))
-    xq, xp = T["xq%d" % mine], T["xp%d" % mine]
+        xdone.append(quant_x(0, q))
+        if q == 0:
+            vec.wait_ge(S.iou, 3)
+            V(lambda: vec.tensor_scalar(T.tmp[:, 0:256], T.j4[:], fr, 2 * FAR, A.not_equal, A.mult))
+            V(lambda: vec.tensor_scalar(T.mk0[:, 4:260], T.tmp[:, 0:256], -FAR, None, A.add))
+        if q == 1:
+            V(lambda: vec.tensor_scalar(base, fq, 256.0, 256.0, A.mult, A.add))
+            V(lambda: vec.tensor_scalar(bnum, base, float(P * rank), None, A.add))
+            V(lambda: vec.memset(T.d1[:], -1.0))
+    source = {1: 0, 2: 0, 3: 3, 4: 3} if ab == 0 else {1: 0, 2: 2, 3: 2, 4: 4}
 
     def score(t):
         for q in range(4):
@@ -200,12 +212,8 @@ def rank_program(g, core, T, topo):
             g.tensor.wait_ge(S["wc%d" % q], t)
             g.tensor.wait_ge(S["ws%d" % q], t)
             i = g.tensor.matmul_mx(T.ps[:, 0:256], T["wc%d" % t][:, 128 * q:128 * q + 128], T["ws%d" % t][:, 128 * q:128 * q + 128],
-                                   xq[:, 256 * q:256 * q + 256], xp[:, 256 * q:256 * q + 256], q == 0, q == 3)
+                                   T.xq0[:, 256 * q:256 * q + 256], T.xp0[:, 256 * q:256 * q + 256], q == 0, q == 3)
         i.then_inc(S.t, 1)
-
-    def source(t, root):
-        k = t if root else t - 1
-        return T["xq%d" % k], T["xp%d" % k]
 
     ydone, wdone = {}, [0]
 
@@ -227,32 +235,44 @@ def rank_program(g, core, T, topo):
     oh_acc, num_acc = [], []
 
     def resolve():
-        pr = tmp(4)
+        pr, nf = tmp(4), tmp(4)
         vec.wait_ge(S.qn, PEER_INC)
-        V(lambda: vec.tensor_tensor(pr, oh_acc[0], T.nl[:, 0:16:4], A.mult))
+        V(lambda: vec.tensor_copy(nf, T.nl[:, 0:32:8]))
+        V(lambda: vec.tensor_tensor(pr, oh_acc[0], nf, A.mult))
         v = V(lambda: vec.tensor_reduce(T.res[:, 0:1], pr, X, A.add))
         g.wait_ge(S.v, v)
         to_mate(T.resl[:, 0:1], T.res[:, 0:1], S.rs)
 
+    def store(t):
+        dq, dp = T["dq%d" % t], T["dp%d" % t]
+        g.sync.dma_start(T.oc[:, 64 * (t - 1):64 * t], u8(dq[:, 128:144])).then_inc(S.st, 16)
+        for k in range(4):
+            g.sync.dma_start(T.osc[4 * k:4 * k + 4, 16 * (t - 1):16 * t], dp[32 * k:32 * k + 4, 128:144]).then_inc(S.st, 16)
+        cnt["st"] += 80
+
     for t in range(1, R + 1):
-        root = (t - 1) % 2 == ab
+        root, flat = (t - 1) % 2 == ab, t == 1
+        merge = root and not flat
         n = "%d" % t
         mk, qm, ym = T["mk" + n], T["qm" + n], T["ym" + n]
+        slot = rank if flat else me
+        nslot = N if flat else nch
+        mq, mp = T["mq" + n], T["mp" + n]
         score(t)
         if t > 1:
             products(t - 1)
         vec.wait_ge(S.t, t)
         V(lambda: vec.tensor_tensor(mk[:, 4:260], T["mk%d" % (t - 1)][:, 4:260], T.ps[:, 0:256], A.max))
-        if root:
+        lo, hi = 4, 260
+        if merge:
             lo, hi = (4, 261) if ab == 0 else (3, 260)
             vec.wait_ge(S["ym" + n], MATE_INC)
-            low = qm[:, 4 * me:4 * me + 1]
-        else:
-            lo, hi = 4, 260
-            low = ym[:, 0:1]
+        low = qm[:, 4 * slot:4 * slot + 1] if flat or root else ym[:, 0:1]
         vm = V(lambda: vec.tensor_reduce(low, mk[:, lo:hi], X, A.min))
         g.wait_ge(S.v, vm)
-        if root:
+        if flat:
+            to_roots(low, low, S["qm" + n], 0)
+        elif root:
             to_peers(low, low, S["qm" + n], 0)
         else:
             c = 260 if ab == 1 else 3
@@ -261,23 +281,31 @@ def rank_program(g, core, T, topo):
         V(lambda: vec.tensor_tensor_scan(T.sc[:, lo:hi], T.d0[:, lo:hi], T.d1[:, lo:hi], BIG, A.min, A.add))
         last = T.sc[:, hi - 1:hi]
         off = T.ofs[:, 4 * t:4 * t + 1]
-        sq, sp = source(t, root)
-        if root:
+        sq, sp = T["xq%d" % source[t]], T["xp%d" % source[t]]
+        if merge:
             e = tmp()
             lim, cmp = (-0.5, A.is_gt) if ab == 0 else (-300.0, A.is_lt)
             V(lambda: vec.tensor_scalar(e, last, lim, dX, cmp, A.mult))
             vo = V(lambda: vec.tensor_scalar(off, last, base, e, A.add, A.add))
-            oq, op, wid = T["mq" + n][:, 16 * me:16 * me + 16], T["mp" + n][:, 16 * me:16 * me + 16], P + 16
+            wid = P + 16
             vec.wait_ge(S["yc" + n], MATE_INC)
             g.scalar.wait_ge(S["ys" + n], MATE_INC)
         else:
             vo = V(lambda: vec.tensor_scalar(off, last, base, None, A.add))
-            oq, op, wid = T["pq" + n][:, 0:16], T["pp" + n][:, 0:16], P
+            wid = P
+        if flat or root:
+            oq, op = mq[:, 16 * slot:16 * slot + 16], mp[:, 16 * slot:16 * slot + 16]
+        else:
+            oq, op = T["pq" + n][:, 0:16], T["pp" + n][:, 0:16]
         vp = V(lambda: vec.tensor_copy(u32(oq), u32(sq[:, 0:wid]).indirect(off)))
         g.scalar.wait_ge(S.v, vo)
         sp_ = AC(lambda: g.scalar.activation(op, sp[:, 0:wid].indirect(off), CP))
         g.wait_ge(S.v, vp)
-        if root:
+        if flat:
+            to_roots(u8(oq), u8(oq), S["qc" + n], 0)
+            g.wait_ge(S.s, sp_)
+            to_roots(op, op, S["qs" + n], 1)
+        elif root:
             to_peers(u8(oq), u8(oq), S["qc" + n], 0)
             g.wait_ge(S.s, sp_)
             to_peers(op, op, S["qs" + n], 1)
@@ -288,49 +316,66 @@ def rank_program(g, core, T, topo):
         if root:
             own, fl, df, num = tmp(), tmp(), tmp(), tmp()
             V(lambda: vec.tensor_scalar(own, last, bnum, None, A.add))
-            V(lambda: vec.tensor_scalar(fl, last, lim, None, cmp))
-            vec.wait_ge(S["yn" + n], MATE_INC)
-            V(lambda: vec.tensor_tensor(df, T["yn" + n][:, 0:1], own, A.subtract))
-            V(lambda: vec.tensor_scalar(num, df, fl, own, A.mult, A.add))
-            if not num_acc:
-                num_acc.append(tmp())
-                V(lambda: vec.tensor_scalar(num_acc[0], num, cf(8 + t), None, A.mult))
-            else:
-                nl = T.nl[:, 4 * me:4 * me + 1]
-                vn = V(lambda: vec.tensor_scalar(nl, num, cf(8 + t), num_acc[0], A.mult, A.add))
-                g.wait_ge(S.v, vn)
-                to_peers(nl, nl, S.qn, 0)
+            if merge:
+                vec.wait_ge(S["yn" + n], MATE_INC)
+                V(lambda: vec.tensor_tensor(df, T["yn" + n][:, 0:1], own, A.subtract))
+                V(lambda: vec.tensor_scalar(fl, last, lim, None, cmp))
+                V(lambda: vec.tensor_scalar(num, df, fl, own, A.mult, A.add))
+                if not num_acc:
+                    num_acc.append(tmp())
+                    V(lambda: vec.tensor_scalar(num_acc[0], num, cf(8 + t), None, A.mult))
+                else:
+                    nl = T.nl[:, 8 * me:8 * me + 1]
+                    vn = V(lambda: vec.tensor_scalar(nl, num, cf(8 + t), num_acc[0], A.mult, A.add))
+                    g.wait_ge(S.v, vn)
+                    to_peers(nl, nl, S.qn, 0)
         else:
             vn = V(lambda: vec.tensor_scalar(ym[:, 1:2], last, bnum, None, A.add))
             g.wait_ge(S.v, vn)
             to_mate(T["yn" + n][:, 0:1], ym[:, 1:2], S["yn" + n])
         if t == 1:
-            vec.wait_ge(S.ld_w, 16)
-            wdone[0] = V(lambda: vec.quantize_mx(T.wq[:, 0:128 * O], T.wp[:, 0:128 * O], T.wb[:, 0:512 * O]))
-            for k in ((3,) if ab == 0 else (2, 4)):
+            V(lambda: vec.memset(T.d1[:, 3:4], -256.0))
+            V(lambda: vec.memset(T.d1[:, 260:261], 0.0))
+            V(lambda: vec.tensor_scalar(b64, fb, 64.0, None, A.add))
+            V(lambda: vec.tensor_scalar(dX, fq, -256.0, fb, A.mult, A.add))
+            V(lambda: vec.tensor_scalar(dX, dX, 768.0 if ab == 0 else 1280.0, None, A.add))
+            for u in range(1, R + 1):
+                if (u - 1) % 2 == ab:
+                    V(lambda: vec.tensor_scalar(cf(8 + u), fg, float(u - 1), None, A.is_equal))
+            for k in sorted(set(source.values()) - {0}):
                 for q in range(4):
                     quant_x(k, q)
+            for u in range(2, R + 1):
+                zeros(u)
+            vec.wait_ge(S.ld_w, 16)
+            wdone[0] = V(lambda: vec.quantize_mx(T.wq[:, 0:128 * O], T.wp[:, 0:128 * O], T.wb[:, 0:512 * O]))
         if t == R and not root:
             resolve()
         dq, dp = T["dq" + n], T["dp" + n]
         if root:
-            rm, d4, s4 = tmp(), tmp(4), tmp(4)
-            vec.wait_ge(S["qm" + n], PEER_INC)
-            V(lambda: vec.tensor_reduce(rm, qm[:, 0:16:4], X, A.min))
-            V(lambda: vec.tensor_scalar(d4, qm[:, 0:16:4], rm, BIG, A.is_gt, A.mult))
-            V(lambda: vec.tensor_tensor_scan(s4, d4, T.d1[:, 4:8], BIG, A.min, A.add))
+            rm, d4, s4 = tmp(), tmp(nslot), tmp(nslot)
+            inc = FLAT_INC if flat else PEER_INC
+            vec.wait_ge(S["qm" + n], inc)
+            V(lambda: vec.tensor_reduce(rm, qm[:, 0:4 * nslot:4], X, A.min))
+            V(lambda: vec.tensor_scalar(d4, qm[:, 0:4 * nslot:4], rm, BIG, A.is_gt, A.mult))
+            V(lambda: vec.tensor_tensor_scan(s4, d4, T.d1[:, 4:4 + nslot], BIG, A.min, A.add))
             i4 = T.tmp[:, tcol[0] - 1:tcol[0]]
             off2 = T.ofs[:, 4 * t + 2:4 * t + 3]
-            vo = V(lambda: vec.tensor_scalar(off2, i4, 16.0, b64, A.mult, A.add))
-            vec.wait_ge(S["qc" + n], PEER_INC)
-            g.scalar.wait_ge(S["qs" + n], PEER_INC)
-            vp = V(lambda: vec.tensor_copy(u32(dq[:, 128:144]), u32(T["mq" + n][:, 0:64]).indirect(off2)))
+            vo = V(lambda: vec.tensor_scalar(off2, i4, 16.0, b128 if flat else b64, A.mult, A.add))
+            vec.wait_ge(S["qc" + n], inc)
+            g.scalar.wait_ge(S["qs" + n], inc)
+            vp = V(lambda: vec.tensor_copy(u32(dq[:, 128:144]), u32(mq[:, 0:16 * nslot]).indirect(off2)))
             g.scalar.wait_ge(S.v, vo)
-            sp_ = AC(lambda: g.scalar.activation(dp[:, 128:144], T["mp" + n][:, 0:64].indirect(off2), CP))
+            sp_ = AC(lambda: g.scalar.activation(dp[:, 128:144], mp[:, 0:16 * nslot].indirect(off2), CP))
             g.wait_ge(S.v, vp)
-            to_mate(u8(dq[:, 128:144]), u8(dq[:, 128:144]), S["dc" + n])
-            g.wait_ge(S.s, sp_)
-            to_mate(dp[:, 128:144], dp[:, 128:144], S["ds" + n])
+            if ab == 0:
+                g.wait_ge(S.s, sp_)
+                fused([(mate, ES[0:4], u8(dq[:, 128:144]), u8(dq[:, 128:144]), S["dc" + n]),
+                       (mate, ES[4:8], dp[:, 80:144], dp[:, 80:144], S["ds" + n])])
+            else:
+                to_mate(u8(dq[:, 128:144]), u8(dq[:, 128:144]), S["dc" + n])
+                g.wait_ge(S.s, sp_)
+                to_mate(dp[:, 128:144], dp[:, 128:144], S["ds" + n])
             vec.wait_ge(S.v, vp)
             cnt["vw"] = cnt["v"]
             g.scalar.wait_ge(S.s, sp_)
@@ -340,24 +385,36 @@ def rank_program(g, core, T, topo):
             if t == R:
                 g.tensor.wait_ge(S.v, vp)
                 g.tensor.wait_ge(S.s, sp_)
-        else:
-            if t < R:
-                vec.wait_ge(S["dc" + n], MATE_INC)
-                g.scalar.wait_ge(S["ds" + n], MATE_INC)
             else:
-                g.tensor.wait_ge(S["dc" + n], MATE_INC)
-                g.tensor.wait_ge(S["ds" + n], MATE_INC)
-            g.sync.wait_ge(S["dc" + n], MATE_INC)
-            g.sync.wait_ge(S["ds" + n], MATE_INC)
+                g.sync.wait_ge(S.t, t + 1)
+        else:
+            inc = 8 if ab == 0 else 4
+            if t < R:
+                vec.wait_ge(S["dc" + n], inc)
+                g.scalar.wait_ge(S["ds" + n], inc)
+            else:
+                g.tensor.wait_ge(S["dc" + n], inc)
+                g.tensor.wait_ge(S["ds" + n], inc)
+            g.sync.wait_ge(S["dc" + n], inc)
+            g.sync.wait_ge(S["ds" + n], inc)
         if t < R:
             windows(t + 1)
-        g.sync.dma_start(T.oc[:, 64 * (t - 1):64 * t], u8(dq[:, 128:144])).then_inc(S.st, 16)
-        for k in range(4):
-            g.sync.dma_start(T.osc[4 * k:4 * k + 4, 16 * (t - 1):16 * t], dp[32 * k:32 * k + 4, 128:144]).then_inc(S.st, 16)
-        cnt["st"] += 80
+        store(t)
         if root:
             oh = tmp(4)
-            V(lambda: vec.tensor_scalar(oh, T.c4[:], i4, cf(8 + t), A.is_equal, A.mult))
+            if flat:
+                d, dd = tmp(4), tmp(4)
+                vec.wait_ge(S["yn" + n], MATE_INC)
+                V(lambda: vec.tensor_tensor(df, T["yn" + n][:, 0:1], own, A.subtract))
+                V(lambda: vec.tensor_scalar(fl, i4, float(2 * me + 1 - N), None, A.is_equal))
+                V(lambda: vec.tensor_scalar(num, df, fl, own, A.mult, A.add))
+                num_acc.append(tmp())
+                V(lambda: vec.tensor_scalar(num_acc[0], num, cf(8 + t), None, A.mult))
+                V(lambda: vec.tensor_scalar(d, T.c8[:], i4, 0.5, A.subtract, A.add))
+                V(lambda: vec.tensor_tensor(dd, d, d, A.mult))
+                V(lambda: vec.tensor_scalar(oh, dd, 1.0, cf(8 + t), A.is_lt, A.mult))
+            else:
+                V(lambda: vec.tensor_scalar(oh, T.c4[:], i4, cf(8 + t), A.is_equal, A.mult))
             if not oh_acc:
                 oh_acc.append(oh)
             else:

@@ -23,13 +23,12 @@ SCRATCH = {
     "nl": ("sbuf", [128, 32], "uint16"),
     "res": ("sbuf", [128, 4], "float32"),
     "resl": ("sbuf", [128, 4], "float32"),
-    "nbv": ("sbuf", [128, 4], "float32"),
     "ysb": ("sbuf", [128, 64 * O], "float32"),
     "ps": ("psum", [128, 512], "float32"),
 }
 for _t in range(R + 1):
     SCRATCH["xq%d" % _t] = ("sbuf", [128, P + 16], F8)
-    SCRATCH["xp%d" % _t] = ("sbuf", [128, P + 16], "uint8")
+    SCRATCH["xp%d" % _t] = ("sbuf", [128, P + 64], "uint8")
     SCRATCH["dq%d" % _t] = ("sbuf", [128, 144], F8)
     SCRATCH["dp%d" % _t] = ("sbuf", [128, 144], "uint8")
     SCRATCH["mk%d" % _t] = ("sbuf", [128, 264], "float32")
@@ -37,8 +36,8 @@ for _t in range(R + 1):
         _m = N if _t == 1 else N // 2
         SCRATCH["wc%d" % _t] = ("sbuf", [128, 512], F8)
         SCRATCH["ws%d" % _t] = ("sbuf", [128, 512], "uint8")
-        SCRATCH["pq%d" % _t] = ("sbuf", [128, 16], F8)
-        SCRATCH["pp%d" % _t] = ("sbuf", [128, 16], "uint8")
+        SCRATCH["pq%d" % _t] = ("sbuf", [128, 144], F8)
+        SCRATCH["pp%d" % _t] = ("sbuf", [128, 144], "uint8")
         SCRATCH["mq%d" % _t] = ("sbuf", [128, 16 * _m], F8)
         SCRATCH["mp%d" % _t] = ("sbuf", [128, 16 * _m], "uint8")
         SCRATCH["qm%d" % _t] = ("sbuf", [128, 4 * _m], "float32")
@@ -101,20 +100,20 @@ def rank_program(g, core, T, topo):
         return DstId(rid=a[0], pnc=a[1])
 
     ES = topo.engines(core, peers[0])[:8]
+    EM = topo.engines(core, mate)[:16]
+    MATE_INC, HALF_INC = len(EM), len(EM) // 2
+    PEER_INC = 8
+    FLAT_INC = 16
 
     def to_mate(out, in_, sem):
         rid, pid = topo.addr(mate)[:2]
-        g.remote_dma(out, in_, sem, S.ls, pid, rid, bits(ES))
-        cnt["ls"] += len(ES)
+        g.remote_dma(out, in_, sem, S.ls, pid, rid, bits(EM))
+        cnt["ls"] += len(EM)
 
     def fused(parts):
         g.remote_dma_fused([RemoteDMATransfer(dst_ids=[dst(c)], dma_engine_mask=bits(e), remote_sem=sem, src=in_, dst=out)
                             for c, e, out, in_, sem in parts], local_sem=S.ls)
         cnt["ls"] += sum(len(p[1]) for p in parts)
-
-    MATE_INC = 8
-    PEER_INC = 8
-    FLAT_INC = 16
 
     def to_peers(out, in_, sem, turn):
         cut = [ES[0:4], ES[4:6], ES[6:8]] if turn == 0 else [ES[4:8], ES[0:2], ES[2:4]]
@@ -158,8 +157,8 @@ def rank_program(g, core, T, topo):
     def cf(k):
         return T.cf[:, k:k + 1]
 
-    def zeros(t):
-        V(lambda: vec.quantize_mx(T["dq%d" % t][:, 0:128], T["dp%d" % t][:, 0:128], T.sd[:, 0:512]))
+    def zeros(name, t, a):
+        return V(lambda: vec.quantize_mx(T["%sq%d" % (name, t)][:, a:a + 128], T["%sp%d" % (name, t)][:, a:a + 128], T.sd[:, 0:512]))
 
     V(lambda: vec.memset(T.sd[:, 0:512], 0.0))
     vec.wait_ge(S.iot, 2)
@@ -172,7 +171,6 @@ def rank_program(g, core, T, topo):
     b128, b64, base, bnum, dX = cf(4), cf(5), cf(6), cf(7), cf(8)
     V(lambda: vec.tensor_scalar(b128, fb, 128.0, None, A.add))
     V(lambda: vec.tensor_scalar(T.cl[:], T.q32[:], fq, b128, A.is_equal, A.mult))
-    zeros(1)
     vec.wait_ge(S.ld_s, 16)
     d0_done = V(lambda: vec.quantize_mx(T.dq0[:, 0:144], T.dp0[:, 0:144], T.sd[:, 0:576]))
 
@@ -228,11 +226,23 @@ def rank_program(g, core, T, topo):
                                T["dq%d" % t][:, 16:144], T["dp%d" % t][:, 16:144], True, True).then_inc(S.ty, 1)
             cnt["ty"] += 1
         g.scalar.wait_ge(S.ty, cnt["ty"])
+        both = t == R and ab == 0
+        if both:
+            vec.wait_ge(S.ty, cnt["ty"])
         for o in range(O):
-            ydone[t] = AC(lambda: g.scalar.activation(T.ysb[:, 64 * o + 16 * (t - 1):64 * o + 16 * t],
-                                                      T["py%d" % (k + o)][:, 112:128], CP))
+            out, in_ = T.ysb[:, 64 * o + 16 * (t - 1):64 * o + 16 * t], T["py%d" % (k + o)][:, 112:128]
+            if both and o == 1:
+                g.scalar.wait_ge(S.v, V(lambda: vec.tensor_copy(out, in_)))
+            else:
+                ydone[t] = AC(lambda: g.scalar.activation(out, in_, CP))
 
     oh_acc, num_acc = [], []
+
+    def rows(buf, which):
+        for k in range(R):
+            if k % 2 == which:
+                g.sync.dma_start(T.nb[k:k + 1, :], buf[16 * k:16 * k + 16, 0:1]).then_inc(S.st, 16)
+                cnt["st"] += 16
 
     def resolve():
         pr, nf = tmp(4), tmp(4)
@@ -242,6 +252,8 @@ def rank_program(g, core, T, topo):
         v = V(lambda: vec.tensor_reduce(T.res[:, 0:1], pr, X, A.add))
         g.wait_ge(S.v, v)
         to_mate(T.resl[:, 0:1], T.res[:, 0:1], S.rs)
+        g.sync.wait_ge(S.v, v)
+        rows(T.res, ab)
 
     def store(t):
         dq, dp = T["dq%d" % t], T["dp%d" % t]
@@ -259,8 +271,6 @@ def rank_program(g, core, T, topo):
         nslot = N if flat else nch
         mq, mp = T["mq" + n], T["mp" + n]
         score(t)
-        if t > 1:
-            products(t - 1)
         vec.wait_ge(S.t, t)
         V(lambda: vec.tensor_tensor(mk[:, 4:260], T["mk%d" % (t - 1)][:, 4:260], T.ps[:, 0:256], A.max))
         lo, hi = 4, 260
@@ -288,8 +298,9 @@ def rank_program(g, core, T, topo):
             V(lambda: vec.tensor_scalar(e, last, lim, dX, cmp, A.mult))
             vo = V(lambda: vec.tensor_scalar(off, last, base, e, A.add, A.add))
             wid = P + 16
-            vec.wait_ge(S["yc" + n], MATE_INC)
-            g.scalar.wait_ge(S["ys" + n], MATE_INC)
+            inc = HALF_INC if ab == 1 else MATE_INC
+            vec.wait_ge(S["yc" + n], inc)
+            g.scalar.wait_ge(S["ys" + n], inc)
         else:
             vo = V(lambda: vec.tensor_scalar(off, last, base, None, A.add))
             wid = P
@@ -302,13 +313,17 @@ def rank_program(g, core, T, topo):
         sp_ = AC(lambda: g.scalar.activation(op, sp[:, 0:wid].indirect(off), CP))
         g.wait_ge(S.v, vp)
         if flat:
-            to_roots(u8(oq), u8(oq), S["qc" + n], 0)
+            to_roots(u8(oq), u8(oq), S["qc" + n], 1)
             g.wait_ge(S.s, sp_)
-            to_roots(op, op, S["qs" + n], 1)
+            to_roots(op, op, S["qs" + n], 0)
         elif root:
-            to_peers(u8(oq), u8(oq), S["qc" + n], 0)
+            to_peers(u8(oq), u8(oq), S["qc" + n], 1)
             g.wait_ge(S.s, sp_)
-            to_peers(op, op, S["qs" + n], 1)
+            to_peers(op, op, S["qs" + n], 0)
+        elif ab == 0:
+            g.wait_ge(S.s, sp_)
+            fused([(mate, EM[:HALF_INC], u8(T["xq" + n][:, P:P + 16]), u8(oq), S["yc" + n]),
+                   (mate, EM[HALF_INC:], T["xp" + n][:, P:P + 64], T["pp" + n][:, 0:64], S["ys" + n])])
         else:
             to_mate(u8(T["xq" + n][:, P:P + 16]), u8(oq), S["yc" + n])
             g.wait_ge(S.s, sp_)
@@ -328,27 +343,37 @@ def rank_program(g, core, T, topo):
                     nl = T.nl[:, 8 * me:8 * me + 1]
                     vn = V(lambda: vec.tensor_scalar(nl, num, cf(8 + t), num_acc[0], A.mult, A.add))
                     g.wait_ge(S.v, vn)
-                    to_peers(nl, nl, S.qn, 0)
+                    to_peers(nl, nl, S.qn, 1)
         else:
             vn = V(lambda: vec.tensor_scalar(ym[:, 1:2], last, bnum, None, A.add))
             g.wait_ge(S.v, vn)
             to_mate(T["yn" + n][:, 0:1], ym[:, 1:2], S["yn" + n])
         if t == 1:
+            zd = zeros("d", 1, 0)
             V(lambda: vec.memset(T.d1[:, 3:4], -256.0))
             V(lambda: vec.memset(T.d1[:, 260:261], 0.0))
             V(lambda: vec.tensor_scalar(b64, fb, 64.0, None, A.add))
             V(lambda: vec.tensor_scalar(dX, fq, -256.0, fb, A.mult, A.add))
-            V(lambda: vec.tensor_scalar(dX, dX, 768.0 if ab == 0 else 1280.0, None, A.add))
+            V(lambda: vec.tensor_scalar(dX, dX, float(P - 256 if ab == 0 else P + 256), None, A.add))
             for u in range(1, R + 1):
                 if (u - 1) % 2 == ab:
                     V(lambda: vec.tensor_scalar(cf(8 + u), fg, float(u - 1), None, A.is_equal))
+            if ab == 0:
+                zeros("p", 2, 16)
+            g.scalar.wait_ge(S.v, zd)
+        if t == (2 if ab == 0 else 1):
+            for u in range(2, R + 1):
+                zd = zeros("d", u, 0)
+            if ab == 0:
+                zd = zeros("p", 4, 16)
             for k in sorted(set(source.values()) - {0}):
                 for q in range(4):
                     quant_x(k, q)
-            for u in range(2, R + 1):
-                zeros(u)
             vec.wait_ge(S.ld_w, 16)
             wdone[0] = V(lambda: vec.quantize_mx(T.wq[:, 0:128 * O], T.wp[:, 0:128 * O], T.wb[:, 0:512 * O]))
+            g.scalar.wait_ge(S.v, zd)
+        if t > 1:
+            products(t - 1)
         if t == R and not root:
             resolve()
         dq, dp = T["dq" + n], T["dp" + n]
@@ -368,38 +393,38 @@ def rank_program(g, core, T, topo):
             g.scalar.wait_ge(S.v, vo)
             sp_ = AC(lambda: g.scalar.activation(dp[:, 128:144], mp[:, 0:16 * nslot].indirect(off2), CP))
             g.wait_ge(S.v, vp)
-            if ab == 0:
-                g.wait_ge(S.s, sp_)
-                fused([(mate, ES[0:4], u8(dq[:, 128:144]), u8(dq[:, 128:144]), S["dc" + n]),
-                       (mate, ES[4:8], dp[:, 80:144], dp[:, 80:144], S["ds" + n])])
-            else:
-                to_mate(u8(dq[:, 128:144]), u8(dq[:, 128:144]), S["dc" + n])
-                g.wait_ge(S.s, sp_)
-                to_mate(dp[:, 128:144], dp[:, 128:144], S["ds" + n])
+            to_mate(u8(dq[:, 128:144]), u8(dq[:, 128:144]), S["dc" + n])
+            g.wait_ge(S.s, sp_)
+            to_mate(dp[:, 128:144], dp[:, 128:144], S["ds" + n])
             vec.wait_ge(S.v, vp)
             cnt["vw"] = cnt["v"]
             g.scalar.wait_ge(S.s, sp_)
             cnt["sw"] = cnt["s"]
-            g.sync.wait_ge(S.v, vp)
-            g.sync.wait_ge(S.s, sp_)
             if t == R:
                 g.tensor.wait_ge(S.v, vp)
                 g.tensor.wait_ge(S.s, sp_)
-            else:
+                g.sync.wait_ge(S.rs, MATE_INC)
+                rows(T.resl, 1 - ab)
+            g.sync.wait_ge(S.v, vp)
+            g.sync.wait_ge(S.s, sp_)
+            if t < R:
                 g.sync.wait_ge(S.t, t + 1)
         else:
-            inc = 8 if ab == 0 else 4
             if t < R:
-                vec.wait_ge(S["dc" + n], inc)
-                g.scalar.wait_ge(S["ds" + n], inc)
+                vec.wait_ge(S["dc" + n], MATE_INC)
+                g.scalar.wait_ge(S["ds" + n], MATE_INC)
             else:
-                g.tensor.wait_ge(S["dc" + n], inc)
-                g.tensor.wait_ge(S["ds" + n], inc)
-            g.sync.wait_ge(S["dc" + n], inc)
-            g.sync.wait_ge(S["ds" + n], inc)
+                g.tensor.wait_ge(S["dc" + n], MATE_INC)
+                g.tensor.wait_ge(S["ds" + n], MATE_INC)
+            g.sync.wait_ge(S["dc" + n], MATE_INC)
+            g.sync.wait_ge(S["ds" + n], MATE_INC)
         if t < R:
             windows(t + 1)
         store(t)
+        if t == R:
+            products(R)
+            g.scalar.wait_ge(S.s, cnt["s"])
+            g.scalar.dma_start(T.y[:], T.ysb[:]).then_inc(S.sty, 16)
         if root:
             oh = tmp(4)
             if flat:
@@ -421,17 +446,11 @@ def rank_program(g, core, T, topo):
                 oh2 = tmp(4)
                 V(lambda: vec.tensor_tensor(oh2, oh, oh_acc[0], A.add))
                 oh_acc[0] = oh2
-        if t == R:
-            products(R)
-            g.scalar.wait_ge(S.s, cnt["s"])
-            g.scalar.dma_start(T.y[:], T.ysb[:]).then_inc(S.sty, 16)
-            if root:
+            if t == R:
                 resolve()
-    vec.wait_ge(S.rs, MATE_INC)
-    vnb = V(lambda: vec.tensor_tensor(T.nbv[:, 0:1], T.res[:, 0:1], T.resl[:, 0:1], A.add))
-    g.sync.wait_ge(S.v, vnb)
-    g.sync.dma_start(T.nb[:], T.nbv[0:64, 0:1]).then_inc(S.st, 16)
-    cnt["st"] += 16
+    if ab == 0:
+        g.sync.wait_ge(S.rs, MATE_INC)
+        rows(T.resl, 1 - ab)
     g.sync.wait_ge(S.st, cnt["st"])
     g.scalar.wait_ge(S.sty, 16)
     g.wait_ge(S.ls, cnt["ls"])

@@ -2,6 +2,7 @@ from concourse.bass import DstId, RemoteDMATransfer
 from concourse.mybir import dt, AluOpType, AxisListType, ActivationFunctionType
 
 R, P, O, N = 4, 1024, 2, 8
+HEAD = 64
 F8 = "float8_e4m3fn_x4"
 SCRATCH = {
     "xb": ("sbuf", [128, 4 * P], "bfloat16"),
@@ -11,13 +12,14 @@ SCRATCH = {
     "ip": ("sbuf", [128, 8], "int32"),
     "q32": ("sbuf", [128, 32], "float32"),
     "j4": ("sbuf", [128, 256], "float32"),
+    "ja": ("sbuf", [128, 256], "float32"),
     "c4": ("sbuf", [128, 4], "float32"),
     "c8": ("sbuf", [128, 4], "float32"),
     "cf": ("sbuf", [128, 16], "float32"),
     "cl": ("sbuf", [128, 32], "uint16"),
-    "d1": ("sbuf", [128, 264], "bfloat16"),
-    "d0": ("sbuf", [128, 264], "bfloat16"),
-    "sc": ("sbuf", [128, 264], "bfloat16"),
+    "d1": ("sbuf", [128, 8], "float32"),
+    "sg": ("sbuf", [128, 256], "bfloat16"),
+    "ct": ("sbuf", [128, 8], "float32"),
     "tmp": ("sbuf", [128, 256], "float32"),
     "ofs": ("sbuf", [128, 32], "uint16"),
     "nl": ("sbuf", [128, 32], "uint16"),
@@ -27,30 +29,33 @@ SCRATCH = {
     "ps": ("psum", [128, 512], "float32"),
 }
 for _t in range(R + 1):
-    SCRATCH["xq%d" % _t] = ("sbuf", [128, P + 16], F8)
-    SCRATCH["xp%d" % _t] = ("sbuf", [128, P + 64], "uint8")
+    SCRATCH["xq%d" % _t] = ("sbuf", [128, HEAD + P], F8)
+    SCRATCH["xp%d" % _t] = ("sbuf", [128, HEAD + P], "uint8")
     SCRATCH["dq%d" % _t] = ("sbuf", [128, 144], F8)
     SCRATCH["dp%d" % _t] = ("sbuf", [128, 144], "uint8")
-    SCRATCH["mk%d" % _t] = ("sbuf", [128, 264], "float32")
+    SCRATCH["mk%d" % _t] = ("sbuf", [128, 256], "float32")
     if _t:
         _m = N if _t == 1 else N // 2
+        SCRATCH["rn%d" % _t] = ("sbuf", [128, 256], "float32")
         SCRATCH["wc%d" % _t] = ("sbuf", [128, 512], F8)
         SCRATCH["ws%d" % _t] = ("sbuf", [128, 512], "uint8")
-        SCRATCH["pq%d" % _t] = ("sbuf", [128, 144], F8)
-        SCRATCH["pp%d" % _t] = ("sbuf", [128, 144], "uint8")
+        SCRATCH["pq%d" % _t] = ("sbuf", [128, 16], F8)
+        SCRATCH["pp%d" % _t] = ("sbuf", [128, 16], "uint8")
         SCRATCH["mq%d" % _t] = ("sbuf", [128, 16 * _m], F8)
         SCRATCH["mp%d" % _t] = ("sbuf", [128, 16 * _m], "uint8")
         SCRATCH["qm%d" % _t] = ("sbuf", [128, 4 * _m], "float32")
+        SCRATCH["yo%d" % _t] = ("sbuf", [128, 4], "float32")
         SCRATCH["ym%d" % _t] = ("sbuf", [128, 4], "float32")
         SCRATCH["yn%d" % _t] = ("sbuf", [128, 4], "float32")
 for _k in range(6):
     SCRATCH["py%d" % _k] = ("psum", [128, 512], "float32")
 SEMAPHORES = ["v", "s", "t", "ty", "iot", "iou", "ls", "ld_s", "ld_w", "st", "sty", "qn", "rs"]
-SEMAPHORES += ["ld%d" % q for q in range(4)] + ["wc%d" % q for q in range(4)] + ["ws%d" % q for q in range(4)]
+SEMAPHORES += ["ld%d" % q for q in range(5)] + ["wc%d" % q for q in range(4)] + ["ws%d" % q for q in range(4)]
 SEMAPHORES += [n + "%d" % t for t in range(1, R + 1) for n in ("ym", "yn", "yc", "ys", "qm", "qc", "qs", "dc", "ds")]
 
 BIG = 4096.0
 FAR = 1e29
+OUT = 8192.0
 
 
 def rank_program(g, core, T, topo):
@@ -59,7 +64,8 @@ def rank_program(g, core, T, topo):
         return
     A = AluOpType
     X = AxisListType.X
-    CP = ActivationFunctionType.Copy
+    ACT = ActivationFunctionType
+    CP, ID = ACT.Copy, ACT.Identity
     S = T.sem
     chips, ranks_of = [], {}
     for c in T.cores:
@@ -76,10 +82,11 @@ def rank_program(g, core, T, topo):
 
     cnt = {"v": 0, "vw": 0, "s": 0, "sw": 0, "ty": 0, "ls": 0, "st": 0}
 
-    def V(call):
-        if cnt["vw"] < cnt["v"]:
-            g.vector.wait_ge(S.v, cnt["v"])
-            cnt["vw"] = cnt["v"]
+    def V(call, after=None):
+        need = cnt["v"] if after is None else after
+        if cnt["vw"] < need:
+            g.vector.wait_ge(S.v, need)
+            cnt["vw"] = need
         call().then_inc(S.v, 1)
         cnt["v"] += 1
         return cnt["v"]
@@ -101,30 +108,33 @@ def rank_program(g, core, T, topo):
 
     ES = topo.engines(core, peers[0])[:8]
     EM = topo.engines(core, mate)[:16]
-    MATE_INC, HALF_INC = len(EM), len(EM) // 2
+    EO = [e for e in EM if e not in ES][:8]
+    MATE_INC = len(EM)
     PEER_INC = 8
-    FLAT_INC = 16
+    FLAT_INC = 16 + len(EO)
+    last_es = EO
 
-    def to_mate(out, in_, sem):
+    def to_mate(out, in_, sem, es=None):
+        es = EM if es is None else es
         rid, pid = topo.addr(mate)[:2]
-        g.remote_dma(out, in_, sem, S.ls, pid, rid, bits(EM))
-        cnt["ls"] += len(EM)
+        g.remote_dma(out, in_, sem, S.ls, pid, rid, bits(es))
+        cnt["ls"] += len(es)
 
     def fused(parts):
         g.remote_dma_fused([RemoteDMATransfer(dst_ids=[dst(c)], dma_engine_mask=bits(e), remote_sem=sem, src=in_, dst=out)
                             for c, e, out, in_, sem in parts], local_sem=S.ls)
         cnt["ls"] += sum(len(p[1]) for p in parts)
 
+    def cuts(turn):
+        return [ES[0:4], ES[4:6], ES[6:8]] if turn == 0 else [ES[4:8], ES[0:2], ES[2:4]]
+
     def to_peers(out, in_, sem, turn):
-        cut = [ES[0:4], ES[4:6], ES[6:8]] if turn == 0 else [ES[4:8], ES[0:2], ES[2:4]]
-        fused([(c, e, out, in_, sem) for c, e in zip(peers, cut)])
+        fused([(c, e, out, in_, sem) for c, e in zip(peers, cuts(turn))])
 
     def to_roots(out, in_, sem, turn):
-        if ab == 0:
-            to_peers(out, in_, sem, turn)
-        else:
-            to = [ranks_of[h][0] for h in others] + [mate]
-            fused([(c, ES[2 * k:2 * k + 2], out, in_, sem) for k, c in enumerate(to)])
+        roots = [ranks_of[h][0] for h in others]
+        parts = [(c, e, out, in_, sem) for c, e in zip(roots, cuts(turn))]
+        fused(parts if ab == 0 else parts + [(mate, EO, out, in_, sem)])
 
     def u8(ap):
         return ap.bitcast(dt.uint8)
@@ -140,12 +150,15 @@ def rank_program(g, core, T, topo):
         return T.tmp[:, a:a + n]
 
     vec = g.vector
+    act = g.scalar.activation
+    cols = [(0, 256), (256, 256), (512, 256), (768, 128), (896, 128)]
     g.sync.dma_start(T.sd[:, 512:576], T.seed[:]).then_inc(S.ld_s, 16)
-    for q in (0, 2):
-        g.sync.dma_start(T.xb[:, 1024 * q:1024 * q + 1024], T.x[:, 1024 * q:1024 * q + 1024]).then_inc(S["ld%d" % q], 16)
-    for q in (1, 3):
-        g.scalar.dma_start(T.xb[:, 1024 * q:1024 * q + 1024], T.x[:, 1024 * q:1024 * q + 1024]).then_inc(S["ld%d" % q], 16)
+    for k in range(5):
+        a, n = cols[k]
+        queue = g.sync if k % 2 == 0 else g.scalar
+        queue.dma_start(T.xb[:, 4 * a:4 * (a + n)], T.x[:, 4 * a:4 * (a + n)]).then_inc(S["ld%d" % k], 16)
     g.sync.wait_ge(S.ld3, 16)
+    g.sync.wait_ge(S.ld4, 16)
     g.sync.dma_start(T.wb[:], T.w[:]).then_inc(S.ld_w, 16)
 
     g.iota(T.ip[:, 0:1], [[0, 1]], 0, 1).then_inc(S.iot, 1)
@@ -157,8 +170,8 @@ def rank_program(g, core, T, topo):
     def cf(k):
         return T.cf[:, k:k + 1]
 
-    def zeros(name, t, a):
-        return V(lambda: vec.quantize_mx(T["%sq%d" % (name, t)][:, a:a + 128], T["%sp%d" % (name, t)][:, a:a + 128], T.sd[:, 0:512]))
+    def zeros(t):
+        return V(lambda: vec.quantize_mx(T["dq%d" % t][:, 0:128], T["dp%d" % t][:, 0:128], T.sd[:, 0:512]))
 
     V(lambda: vec.memset(T.sd[:, 0:512], 0.0))
     vec.wait_ge(S.iot, 2)
@@ -168,39 +181,50 @@ def rank_program(g, core, T, topo):
     V(lambda: vec.tensor_scalar(T.ip[:, 4:5], T.ip[:, 0:1], 4, None, A.logical_shift_right))
     V(lambda: vec.tensor_copy(T.cf[:, 0:4], T.ip[:, 1:5]))
     fb, fq, fr, fg = cf(0), cf(1), cf(2), cf(3)
-    b128, b64, base, bnum, dX = cf(4), cf(5), cf(6), cf(7), cf(8)
+    b128, b64, base, bnum = cf(4), cf(5), cf(6), cf(7)
     V(lambda: vec.tensor_scalar(b128, fb, 128.0, None, A.add))
     V(lambda: vec.tensor_scalar(T.cl[:], T.q32[:], fq, b128, A.is_equal, A.mult))
+    V(lambda: vec.memset(T.d1[:], -1.0))
+    for u in range(1, R + 1):
+        if (u - 1) % 2 == ab:
+            V(lambda: vec.tensor_scalar(cf(8 + u), fg, float(u - 1), None, A.is_equal))
+    if ab == 0:
+        zeros(1)
     vec.wait_ge(S.ld_s, 16)
     d0_done = V(lambda: vec.quantize_mx(T.dq0[:, 0:144], T.dp0[:, 0:144], T.sd[:, 0:576]))
 
-    def windows(t):
+    def windows(t, sready=None):
         q0, p0, wc, ws = T["dq%d" % (t - 1)], T["dp%d" % (t - 1)], T["wc%d" % t], T["ws%d" % t]
         for q in range(4):
             vec.tensor_copy(u32(wc[:, 128 * q:128 * q + 128]), u32(q0[:, 0:144]).indirect(T.cl[:, 8 * q:8 * q + 8])).then_inc(S["wc%d" % q], 1)
-            g.scalar.activation(ws[:, 128 * q:128 * q + 128], p0[:, 0:144].indirect(T.cl[:, 8 * q:8 * q + 8]), CP).then_inc(S["ws%d" % q], 1)
+            if q < 3:
+                act(ws[:, 128 * q:128 * q + 128], p0[:, 0:144].indirect(T.cl[:, 8 * q:8 * q + 8]), CP).then_inc(S["ws%d" % q], 1)
+        if sready:
+            vec.wait_ge(sready[0], sready[1])
+        vec.tensor_copy(ws[:, 384:512], p0[:, 0:144].indirect(T.cl[:, 24:32])).then_inc(S.ws3, 1)
 
     vec.wait_ge(S.v, d0_done)
     cnt["vw"] = cnt["v"]
     g.scalar.wait_ge(S.v, d0_done)
     windows(1)
 
-    def quant_x(k, q):
-        return V(lambda: vec.quantize_mx(T["xq%d" % k][:, 256 * q:256 * q + 256], T["xp%d" % k][:, 256 * q:256 * q + 256],
-                                         T.xb[:, 1024 * q:1024 * q + 1024]))
+    g.scalar.wait_ge(S.iou, 3)
+    AC(lambda: act(base, fq, ID, bias=float(HEAD), scale=256.0))
+    AC(lambda: act(bnum, fq, ID, bias=float(P * rank), scale=256.0))
+    AC(lambda: act(b64, fb, ID, bias=64.0))
+    AC(lambda: act(T.ja[:], T.j4[:], ACT.Abs, bias=fr, scale=-1.0))
+    consts = AC(lambda: act(T.mk0[:], T.ja[:], ID, bias=-FAR, scale=2 * FAR))
+
+    def quant_x(k, a, n):
+        return V(lambda: vec.quantize_mx(T["xq%d" % k][:, HEAD + a:HEAD + a + n], T["xp%d" % k][:, HEAD + a:HEAD + a + n],
+                                         T.xb[:, 4 * a:4 * (a + n)]))
 
     xdone = []
-    for q in range(4):
-        vec.wait_ge(S["ld%d" % q], 16)
-        xdone.append(quant_x(0, q))
-        if q == 0:
-            vec.wait_ge(S.iou, 3)
-            V(lambda: vec.tensor_scalar(T.tmp[:, 0:256], T.j4[:], fr, 2 * FAR, A.not_equal, A.mult))
-            V(lambda: vec.tensor_scalar(T.mk0[:, 4:260], T.tmp[:, 0:256], -FAR, None, A.add))
-        if q == 1:
-            V(lambda: vec.tensor_scalar(base, fq, 256.0, 256.0, A.mult, A.add))
-            V(lambda: vec.tensor_scalar(bnum, base, float(P * rank), None, A.add))
-            V(lambda: vec.memset(T.d1[:], -1.0))
+    for k in range(5):
+        vec.wait_ge(S["ld%d" % k], 16)
+        xdone.append(quant_x(0, *cols[k]))
+    xdone[3] = xdone[4]
+    vec.wait_ge(S.s, consts)
     source = {1: 0, 2: 0, 3: 3, 4: 3} if ab == 0 else {1: 0, 2: 2, 3: 2, 4: 4}
 
     def score(t):
@@ -209,8 +233,9 @@ def rank_program(g, core, T, topo):
                 g.tensor.wait_ge(S.v, xdone[q])
             g.tensor.wait_ge(S["wc%d" % q], t)
             g.tensor.wait_ge(S["ws%d" % q], t)
+            a = HEAD + 256 * q
             i = g.tensor.matmul_mx(T.ps[:, 0:256], T["wc%d" % t][:, 128 * q:128 * q + 128], T["ws%d" % t][:, 128 * q:128 * q + 128],
-                                   T.xq0[:, 256 * q:256 * q + 256], T.xp0[:, 256 * q:256 * q + 256], q == 0, q == 3)
+                                   T.xq0[:, a:a + 256], T.xp0[:, a:a + 256], q == 0, q == 3)
         i.then_inc(S.t, 1)
 
     ydone, wdone = {}, [0]
@@ -234,7 +259,7 @@ def rank_program(g, core, T, topo):
             if both and o == 1:
                 g.scalar.wait_ge(S.v, V(lambda: vec.tensor_copy(out, in_)))
             else:
-                ydone[t] = AC(lambda: g.scalar.activation(out, in_, CP))
+                ydone[t] = AC(lambda: act(out, in_, CP))
 
     oh_acc, num_acc = [], []
 
@@ -252,205 +277,206 @@ def rank_program(g, core, T, topo):
         v = V(lambda: vec.tensor_reduce(T.res[:, 0:1], pr, X, A.add))
         g.wait_ge(S.v, v)
         to_mate(T.resl[:, 0:1], T.res[:, 0:1], S.rs)
-        g.sync.wait_ge(S.v, v)
-        rows(T.res, ab)
+        return v
 
-    def store(t):
+    def store(t, codes, scales):
         dq, dp = T["dq%d" % t], T["dp%d" % t]
+        g.sync.wait_ge(*codes)
         g.sync.dma_start(T.oc[:, 64 * (t - 1):64 * t], u8(dq[:, 128:144])).then_inc(S.st, 16)
+        g.sync.wait_ge(*scales)
         for k in range(4):
             g.sync.dma_start(T.osc[4 * k:4 * k + 4, 16 * (t - 1):16 * t], dp[32 * k:32 * k + 4, 128:144]).then_inc(S.st, 16)
         cnt["st"] += 80
 
+    def send_numbers(t, num):
+        nl = T.nl[:, 8 * me:8 * me + 1]
+        g.wait_ge(S.v, V(lambda: vec.tensor_scalar(nl, num, cf(8 + t), num_acc[0], A.mult, A.add)))
+        to_peers(nl, nl, S.qn, 1)
+
+    def which_slot(t, i4):
+        oh = tmp(4)
+        if t == 1:
+            d, dd = tmp(4), tmp(4)
+            V(lambda: vec.tensor_scalar(d, T.c8[:], i4, 0.5, A.subtract, A.add))
+            V(lambda: vec.tensor_tensor(dd, d, d, A.mult))
+            V(lambda: vec.tensor_scalar(oh, dd, 1.0, cf(8 + t), A.is_lt, A.mult))
+        else:
+            V(lambda: vec.tensor_scalar(oh, T.c4[:], i4, cf(8 + t), A.is_equal, A.mult))
+        if not oh_acc:
+            oh_acc.append(oh)
+        else:
+            oh2 = tmp(4)
+            V(lambda: vec.tensor_tensor(oh2, oh, oh_acc[0], A.add))
+            oh_acc[0] = oh2
+
+    def numbers(t, e, i4, ct):
+        own, fl, df, num = tmp(), tmp(), tmp(), tmp()
+        V(lambda: vec.tensor_scalar(own, ct, -1.0, bnum, A.mult, A.add))
+        if t == 1:
+            V(lambda: vec.tensor_scalar(fl, i4, float(2 * me + 1 - N), None, A.is_equal))
+        else:
+            V(lambda: vec.tensor_scalar(fl, e, -1.0 / OUT, None, A.mult))
+        vec.wait_ge(S["yn%d" % t], MATE_INC)
+        V(lambda: vec.tensor_tensor(df, T["yn%d" % t][:, 0:1], own, A.subtract))
+        V(lambda: vec.tensor_scalar(num, df, fl, own, A.mult, A.add))
+        if not num_acc:
+            num_acc.append(tmp())
+            V(lambda: vec.tensor_scalar(num_acc[0], num, cf(8 + t), None, A.mult))
+        else:
+            send_numbers(t, num)
+        which_slot(t, i4)
+
+    later = []
     for t in range(1, R + 1):
         root, flat = (t - 1) % 2 == ab, t == 1
         merge = root and not flat
         n = "%d" % t
-        mk, qm, ym = T["mk" + n], T["qm" + n], T["ym" + n]
+        mk, qm, rn, ct = T["mk" + n], T["qm" + n], T["rn" + n], T.ct[:, t:t + 1]
         slot = rank if flat else me
         nslot = N if flat else nch
         mq, mp = T["mq" + n], T["mp" + n]
         score(t)
         vec.wait_ge(S.t, t)
-        V(lambda: vec.tensor_tensor(mk[:, 4:260], T["mk%d" % (t - 1)][:, 4:260], T.ps[:, 0:256], A.max))
-        lo, hi = 4, 260
-        if merge:
-            lo, hi = (4, 261) if ab == 0 else (3, 260)
-            vec.wait_ge(S["ym" + n], MATE_INC)
-        low = qm[:, 4 * slot:4 * slot + 1] if flat or root else ym[:, 0:1]
-        vm = V(lambda: vec.tensor_reduce(low, mk[:, lo:hi], X, A.min))
-        g.wait_ge(S.v, vm)
-        if flat:
-            to_roots(low, low, S["qm" + n], 0)
-        elif root:
-            to_peers(low, low, S["qm" + n], 0)
-        else:
-            c = 260 if ab == 1 else 3
-            to_mate(mk[:, c:c + 1], low, S["ym" + n])
-        V(lambda: vec.tensor_scalar(T.d0[:, lo:hi], mk[:, lo:hi], low, BIG, A.is_gt, A.mult))
-        V(lambda: vec.tensor_tensor_scan(T.sc[:, lo:hi], T.d0[:, lo:hi], T.d1[:, lo:hi], BIG, A.min, A.add))
-        last = T.sc[:, hi - 1:hi]
+        V(lambda: vec.tensor_tensor(mk[:], T["mk%d" % (t - 1)][:], T.ps[:, 0:256], A.max))
+        vr = V(lambda: vec.tensor_tensor_scan(rn[:], mk[:], mk[:], FAR, A.min, A.min))
+        low = rn[:, 255:256]
+        g.scalar.wait_ge(S.v, vr)
+        sct = AC(lambda: act(T.sg[:], rn[:], ACT.Sign, bias=low, scale=-1.0, accum_out=ct))
         off = T.ofs[:, 4 * t:4 * t + 1]
         sq, sp = T["xq%d" % source[t]], T["xp%d" % source[t]]
+        e = None
         if merge:
-            e = tmp()
-            lim, cmp = (-0.5, A.is_gt) if ab == 0 else (-300.0, A.is_lt)
-            V(lambda: vec.tensor_scalar(e, last, lim, dX, cmp, A.mult))
-            vo = V(lambda: vec.tensor_scalar(off, last, base, e, A.add, A.add))
-            wid = P + 16
-            inc = HALF_INC if ab == 1 else MATE_INC
-            vec.wait_ge(S["yc" + n], inc)
-            g.scalar.wait_ge(S["ys" + n], inc)
+            e, eb = tmp(), tmp()
+            ym, low2 = T["ym" + n][:, 0:1], qm[:, 4 * slot:4 * slot + 1]
+            vec.wait_ge(S["ym" + n], MATE_INC)
+            ve = V(lambda: vec.tensor_scalar(e, ym, low, -OUT, A.is_lt if ab == 0 else A.is_le, A.mult))
+            vm = V(lambda: vec.tensor_tensor(low2, ym, low, A.min), after=vr)
+            vb = V(lambda: vec.tensor_scalar(eb, e, base, None, A.add), after=ve)
+            g.wait_ge(S.v, vm)
+            to_peers(low2, low2, S["qm" + n], 0)
+            vec.wait_ge(S.s, sct)
+            vo = V(lambda: vec.tensor_scalar(off, eb, ct, fb, A.subtract, A.max), after=vb)
+            vec.wait_ge(S["yc" + n], MATE_INC)
         else:
-            vo = V(lambda: vec.tensor_scalar(off, last, base, None, A.add))
-            wid = P
+            g.wait_ge(S.v, vr)
+            if flat:
+                to_roots(qm[:, 4 * slot:4 * slot + 1], low, S["qm" + n], 0)
+                if root:
+                    AC(lambda: act(qm[:, 4 * slot:4 * slot + 1], low, CP))
+            else:
+                to_mate(T["ym" + n][:, 0:1], low, S["ym" + n])
+            vec.wait_ge(S.s, sct)
+            vo = V(lambda: vec.tensor_scalar(off, ct, -1.0, base, A.mult, A.add))
         if flat or root:
             oq, op = mq[:, 16 * slot:16 * slot + 16], mp[:, 16 * slot:16 * slot + 16]
         else:
             oq, op = T["pq" + n][:, 0:16], T["pp" + n][:, 0:16]
-        vp = V(lambda: vec.tensor_copy(u32(oq), u32(sq[:, 0:wid]).indirect(off)))
+        vp = V(lambda: vec.tensor_copy(u32(oq), u32(sq[:, 0:HEAD + P]).indirect(off)))
         g.scalar.wait_ge(S.v, vo)
-        sp_ = AC(lambda: g.scalar.activation(op, sp[:, 0:wid].indirect(off), CP))
+        if merge:
+            g.scalar.wait_ge(S["ys" + n], MATE_INC)
+        own_s = AC(lambda: act(op, sp[:, 0:HEAD + P].indirect(off), CP))
         g.wait_ge(S.v, vp)
         if flat:
             to_roots(u8(oq), u8(oq), S["qc" + n], 1)
-            g.wait_ge(S.s, sp_)
+            g.wait_ge(S.s, own_s)
             to_roots(op, op, S["qs" + n], 0)
         elif root:
             to_peers(u8(oq), u8(oq), S["qc" + n], 1)
-            g.wait_ge(S.s, sp_)
+            g.wait_ge(S.s, own_s)
             to_peers(op, op, S["qs" + n], 0)
-        elif ab == 0:
-            g.wait_ge(S.s, sp_)
-            fused([(mate, EM[:HALF_INC], u8(T["xq" + n][:, P:P + 16]), u8(oq), S["yc" + n]),
-                   (mate, EM[HALF_INC:], T["xp" + n][:, P:P + 64], T["pp" + n][:, 0:64], S["ys" + n])])
         else:
-            to_mate(u8(T["xq" + n][:, P:P + 16]), u8(oq), S["yc" + n])
-            g.wait_ge(S.s, sp_)
-            to_mate(T["xp" + n][:, P:P + 16], op, S["ys" + n])
-        if root:
-            own, fl, df, num = tmp(), tmp(), tmp(), tmp()
-            V(lambda: vec.tensor_scalar(own, last, bnum, None, A.add))
-            if merge:
-                vec.wait_ge(S["yn" + n], MATE_INC)
-                V(lambda: vec.tensor_tensor(df, T["yn" + n][:, 0:1], own, A.subtract))
-                V(lambda: vec.tensor_scalar(fl, last, lim, None, cmp))
-                V(lambda: vec.tensor_scalar(num, df, fl, own, A.mult, A.add))
-                if not num_acc:
-                    num_acc.append(tmp())
-                    V(lambda: vec.tensor_scalar(num_acc[0], num, cf(8 + t), None, A.mult))
-                else:
-                    nl = T.nl[:, 8 * me:8 * me + 1]
-                    vn = V(lambda: vec.tensor_scalar(nl, num, cf(8 + t), num_acc[0], A.mult, A.add))
-                    g.wait_ge(S.v, vn)
-                    to_peers(nl, nl, S.qn, 1)
-        else:
-            vn = V(lambda: vec.tensor_scalar(ym[:, 1:2], last, bnum, None, A.add))
-            g.wait_ge(S.v, vn)
-            to_mate(T["yn" + n][:, 0:1], ym[:, 1:2], S["yn" + n])
-        if t == 1:
-            zd = zeros("d", 1, 0)
-            V(lambda: vec.memset(T.d1[:, 3:4], -256.0))
-            V(lambda: vec.memset(T.d1[:, 260:261], 0.0))
-            V(lambda: vec.tensor_scalar(b64, fb, 64.0, None, A.add))
-            V(lambda: vec.tensor_scalar(dX, fq, -256.0, fb, A.mult, A.add))
-            V(lambda: vec.tensor_scalar(dX, dX, float(P - 256 if ab == 0 else P + 256), None, A.add))
-            for u in range(1, R + 1):
-                if (u - 1) % 2 == ab:
-                    V(lambda: vec.tensor_scalar(cf(8 + u), fg, float(u - 1), None, A.is_equal))
-            if ab == 0:
-                zeros("p", 2, 16)
-            g.scalar.wait_ge(S.v, zd)
-        if t == (2 if ab == 0 else 1):
-            for u in range(2, R + 1):
-                zd = zeros("d", u, 0)
-            if ab == 0:
-                zd = zeros("p", 4, 16)
-            for k in sorted(set(source.values()) - {0}):
-                for q in range(4):
-                    quant_x(k, q)
-            vec.wait_ge(S.ld_w, 16)
-            wdone[0] = V(lambda: vec.quantize_mx(T.wq[:, 0:128 * O], T.wp[:, 0:128 * O], T.wb[:, 0:512 * O]))
-            g.scalar.wait_ge(S.v, zd)
+            to_mate(u8(T["xq" + n][:, 0:16]), u8(oq), S["yc" + n])
+            g.wait_ge(S.s, own_s)
+            to_mate(T["xp" + n][:, 0:16], op, S["ys" + n])
+        if not root:
+            yo = T["yo" + n][:, 0:1]
+            g.wait_ge(S.v, V(lambda: vec.tensor_scalar(yo, ct, -1.0, bnum, A.mult, A.add)))
+            to_mate(T["yn" + n][:, 0:1], yo, S["yn" + n])
+            if t < 3:
+                for u in range(1 if ab == 1 else 2, R + 1):
+                    zd = zeros(u)
+                g.scalar.wait_ge(S.v, zd)
+            if t < R:
+                for c in cols:
+                    quant_x(source[t + 1], *c)
+            if t < 3:
+                vec.wait_ge(S.ld_w, 16)
+                wdone[0] = V(lambda: vec.quantize_mx(T.wq[:, 0:128 * O], T.wp[:, 0:128 * O], T.wb[:, 0:512 * O]))
+            for f in later:
+                f()
+            later = []
         if t > 1:
             products(t - 1)
         if t == R and not root:
-            resolve()
+            g.sync.wait_ge(S.v, resolve())
+            rows(T.res, ab)
         dq, dp = T["dq" + n], T["dp" + n]
+        es = last_es if t == R else EM
         if root:
             rm, d4, s4 = tmp(), tmp(nslot), tmp(nslot)
+            i4 = T.tmp[:, tcol[0] - 1:tcol[0]]
+            if t == R:
+                own, fl, df, num = tmp(), tmp(), tmp(), tmp()
+                vown = V(lambda: vec.tensor_scalar(own, ct, -1.0, bnum, A.mult, A.add), after=vo)
+                V(lambda: vec.tensor_scalar(fl, e, -1.0 / OUT, None, A.mult), after=vo)
+                vec.wait_ge(S["yn" + n], MATE_INC)
+                V(lambda: vec.tensor_tensor(df, T["yn" + n][:, 0:1], own, A.subtract), after=vown)
+                V(lambda: vec.tensor_scalar(num, df, fl, own, A.mult, A.add))
+                send_numbers(t, num)
             inc = FLAT_INC if flat else PEER_INC
             vec.wait_ge(S["qm" + n], inc)
+            if flat:
+                vec.wait_ge(S.s, own_s)
             V(lambda: vec.tensor_reduce(rm, qm[:, 0:4 * nslot:4], X, A.min))
             V(lambda: vec.tensor_scalar(d4, qm[:, 0:4 * nslot:4], rm, BIG, A.is_gt, A.mult))
-            V(lambda: vec.tensor_tensor_scan(s4, d4, T.d1[:, 4:4 + nslot], BIG, A.min, A.add))
-            i4 = T.tmp[:, tcol[0] - 1:tcol[0]]
+            V(lambda: vec.tensor_tensor_scan(s4, d4, T.d1[:, 0:nslot], BIG, A.min, A.add))
             off2 = T.ofs[:, 4 * t + 2:4 * t + 3]
             vo = V(lambda: vec.tensor_scalar(off2, i4, 16.0, b128 if flat else b64, A.mult, A.add))
             vec.wait_ge(S["qc" + n], inc)
             g.scalar.wait_ge(S["qs" + n], inc)
             vp = V(lambda: vec.tensor_copy(u32(dq[:, 128:144]), u32(mq[:, 0:16 * nslot]).indirect(off2)))
             g.scalar.wait_ge(S.v, vo)
-            sp_ = AC(lambda: g.scalar.activation(dp[:, 128:144], mp[:, 0:16 * nslot].indirect(off2), CP))
+            sp_ = AC(lambda: act(dp[:, 128:144], mp[:, 0:16 * nslot].indirect(off2), CP))
             g.wait_ge(S.v, vp)
-            to_mate(u8(dq[:, 128:144]), u8(dq[:, 128:144]), S["dc" + n])
+            to_mate(u8(dq[:, 128:144]), u8(dq[:, 128:144]), S["dc" + n], es)
             g.wait_ge(S.s, sp_)
             to_mate(dp[:, 128:144], dp[:, 128:144], S["ds" + n])
-            vec.wait_ge(S.v, vp)
-            cnt["vw"] = cnt["v"]
-            g.scalar.wait_ge(S.s, sp_)
-            cnt["sw"] = cnt["s"]
-            if t == R:
+            if t < R:
+                vec.wait_ge(S.v, vp)
+                cnt["vw"] = cnt["v"]
+                g.scalar.wait_ge(S.s, sp_)
+                cnt["sw"] = cnt["s"]
+                windows(t + 1, (S.s, sp_))
+                later.append(lambda t=t, e=e, i4=i4, ct=ct: numbers(t, e, i4, ct))
+                g.sync.wait_ge(S.t, t + 1)
+            else:
                 g.tensor.wait_ge(S.v, vp)
                 g.tensor.wait_ge(S.s, sp_)
-                g.sync.wait_ge(S.rs, MATE_INC)
-                rows(T.resl, 1 - ab)
-            g.sync.wait_ge(S.v, vp)
-            g.sync.wait_ge(S.s, sp_)
-            if t < R:
-                g.sync.wait_ge(S.t, t + 1)
+            store(t, (S.v, vp), (S.s, sp_))
+            if t == R:
+                products(R)
+                which_slot(t, i4)
         else:
             if t < R:
-                vec.wait_ge(S["dc" + n], MATE_INC)
+                vec.wait_ge(S["dc" + n], len(es))
                 g.scalar.wait_ge(S["ds" + n], MATE_INC)
+                windows(t + 1, (S["ds" + n], MATE_INC))
             else:
-                g.tensor.wait_ge(S["dc" + n], MATE_INC)
+                g.tensor.wait_ge(S["dc" + n], len(es))
                 g.tensor.wait_ge(S["ds" + n], MATE_INC)
-            g.sync.wait_ge(S["dc" + n], MATE_INC)
-            g.sync.wait_ge(S["ds" + n], MATE_INC)
-        if t < R:
-            windows(t + 1)
-        store(t)
+            store(t, (S["dc" + n], len(es)), (S["ds" + n], MATE_INC))
+            if t == R:
+                products(R)
         if t == R:
-            products(R)
             g.scalar.wait_ge(S.s, cnt["s"])
             g.scalar.dma_start(T.y[:], T.ysb[:]).then_inc(S.sty, 16)
-        if root:
-            oh = tmp(4)
-            if flat:
-                d, dd = tmp(4), tmp(4)
-                vec.wait_ge(S["yn" + n], MATE_INC)
-                V(lambda: vec.tensor_tensor(df, T["yn" + n][:, 0:1], own, A.subtract))
-                V(lambda: vec.tensor_scalar(fl, i4, float(2 * me + 1 - N), None, A.is_equal))
-                V(lambda: vec.tensor_scalar(num, df, fl, own, A.mult, A.add))
-                num_acc.append(tmp())
-                V(lambda: vec.tensor_scalar(num_acc[0], num, cf(8 + t), None, A.mult))
-                V(lambda: vec.tensor_scalar(d, T.c8[:], i4, 0.5, A.subtract, A.add))
-                V(lambda: vec.tensor_tensor(dd, d, d, A.mult))
-                V(lambda: vec.tensor_scalar(oh, dd, 1.0, cf(8 + t), A.is_lt, A.mult))
-            else:
-                V(lambda: vec.tensor_scalar(oh, T.c4[:], i4, cf(8 + t), A.is_equal, A.mult))
-            if not oh_acc:
-                oh_acc.append(oh)
-            else:
-                oh2 = tmp(4)
-                V(lambda: vec.tensor_tensor(oh2, oh, oh_acc[0], A.add))
-                oh_acc[0] = oh2
-            if t == R:
-                resolve()
-    if ab == 0:
-        g.sync.wait_ge(S.rs, MATE_INC)
-        rows(T.resl, 1 - ab)
+            v = resolve() if root else 0
+            g.sync.wait_ge(S.rs, MATE_INC)
+            rows(T.resl, 1 - ab)
+            if root:
+                g.sync.wait_ge(S.v, v)
+                rows(T.res, ab)
     g.sync.wait_ge(S.st, cnt["st"])
     g.scalar.wait_ge(S.sty, 16)
     g.wait_ge(S.ls, cnt["ls"])

@@ -3,6 +3,7 @@ from concourse.mybir import dt, AluOpType, AxisListType, ActivationFunctionType
 
 R, P, O, N = 4, 1024, 2, 8
 HEAD = 64
+ZERO = 128
 F8 = "float8_e4m3fn_x4"
 SCRATCH = {
     "xb": ("sbuf", [128, 4 * P], "bfloat16"),
@@ -17,9 +18,10 @@ SCRATCH = {
     "c8": ("sbuf", [128, 4], "float32"),
     "cf": ("sbuf", [128, 16], "float32"),
     "cl": ("sbuf", [128, 32], "uint16"),
-    "d1": ("sbuf", [128, 8], "float32"),
-    "sg": ("sbuf", [128, 256], "bfloat16"),
+    "sg": ("sbuf", [128, 256 * (R + 1)], "bfloat16"),
+    "sh": ("sbuf", [128, 8 * (R + 1)], "bfloat16"),
     "ct": ("sbuf", [128, 8], "float32"),
+    "ns": ("sbuf", [128, 8], "float32"),
     "tmp": ("sbuf", [128, 256], "float32"),
     "ofs": ("sbuf", [128, 32], "uint16"),
     "nl": ("sbuf", [128, 32], "uint16"),
@@ -31,18 +33,19 @@ SCRATCH = {
 for _t in range(R + 1):
     SCRATCH["xq%d" % _t] = ("sbuf", [128, HEAD + P], F8)
     SCRATCH["xp%d" % _t] = ("sbuf", [128, HEAD + P], "uint8")
-    SCRATCH["dq%d" % _t] = ("sbuf", [128, 144], F8)
-    SCRATCH["dp%d" % _t] = ("sbuf", [128, 144], "uint8")
+    SCRATCH["dq%d" % _t] = ("sbuf", [128, ZERO + 16], F8)
+    SCRATCH["dp%d" % _t] = ("sbuf", [128, ZERO + 16], "uint8")
     SCRATCH["mk%d" % _t] = ("sbuf", [128, 256], "float32")
     if _t:
         _m = N if _t == 1 else N // 2
         SCRATCH["rn%d" % _t] = ("sbuf", [128, 256], "float32")
+        SCRATCH["cm%d" % _t] = ("sbuf", [128, 32], "uint16")
         SCRATCH["wc%d" % _t] = ("sbuf", [128, 512], F8)
         SCRATCH["ws%d" % _t] = ("sbuf", [128, 512], "uint8")
         SCRATCH["pq%d" % _t] = ("sbuf", [128, 16], F8)
         SCRATCH["pp%d" % _t] = ("sbuf", [128, 16], "uint8")
-        SCRATCH["mq%d" % _t] = ("sbuf", [128, 16 * _m], F8)
-        SCRATCH["mp%d" % _t] = ("sbuf", [128, 16 * _m], "uint8")
+        SCRATCH["mq%d" % _t] = ("sbuf", [128, ZERO + 16 * _m], F8)
+        SCRATCH["mp%d" % _t] = ("sbuf", [128, ZERO + 16 * _m], "uint8")
         SCRATCH["qm%d" % _t] = ("sbuf", [128, 4 * _m], "float32")
         SCRATCH["yo%d" % _t] = ("sbuf", [128, 4], "float32")
         SCRATCH["ym%d" % _t] = ("sbuf", [128, 4], "float32")
@@ -53,7 +56,6 @@ SEMAPHORES = ["v", "s", "t", "ty", "iot", "iou", "ls", "ld_s", "ld_w", "st", "st
 SEMAPHORES += ["ld%d" % q for q in range(5)] + ["wc%d" % q for q in range(4)] + ["ws%d" % q for q in range(4)]
 SEMAPHORES += [n + "%d" % t for t in range(1, R + 1) for n in ("ym", "yn", "yc", "ys", "qm", "qc", "qs", "dc", "ds")]
 
-BIG = 4096.0
 FAR = 1e29
 OUT = 8192.0
 
@@ -91,10 +93,10 @@ def rank_program(g, core, T, topo):
         cnt["v"] += 1
         return cnt["v"]
 
-    def AC(call):
-        if cnt["sw"] < cnt["s"]:
-            g.scalar.wait_ge(S.s, cnt["s"])
-            cnt["sw"] = cnt["s"]
+    def AC(call, after=0):
+        if cnt["sw"] < after:
+            g.scalar.wait_ge(S.s, after)
+            cnt["sw"] = after
         call().then_inc(S.s, 1)
         cnt["s"] += 1
         return cnt["s"]
@@ -164,60 +166,59 @@ def rank_program(g, core, T, topo):
     g.iota(T.ip[:, 0:1], [[0, 1]], 0, 1).then_inc(S.iot, 1)
     g.iota(T.q32[:], [[1, 4], [0, 8]], 0, 0, allow_small_or_imprecise_dtypes=True).then_inc(S.iot, 1)
     g.iota(T.j4[:], [[1, 4], [0, 64]], 0, 0, allow_small_or_imprecise_dtypes=True).then_inc(S.iou, 1)
-    g.iota(T.c4[:], [[1, 4]], -4, 0, allow_small_or_imprecise_dtypes=True).then_inc(S.iou, 1)
-    g.iota(T.c8[:], [[2, 4]], -8, 0, allow_small_or_imprecise_dtypes=True).then_inc(S.iou, 1)
+    g.iota(T.c4[:], [[-1, 4]], 0, 0, allow_small_or_imprecise_dtypes=True).then_inc(S.iou, 1)
+    g.iota(T.c8[:], [[-2, 4]], 0, 0, allow_small_or_imprecise_dtypes=True).then_inc(S.iou, 1)
 
     def cf(k):
         return T.cf[:, k:k + 1]
 
-    def zeros(t):
-        return V(lambda: vec.quantize_mx(T["dq%d" % t][:, 0:128], T["dp%d" % t][:, 0:128], T.sd[:, 0:512]))
+    def zeros(name, t):
+        return V(lambda: vec.quantize_mx(T["%sq%d" % (name, t)][:, 0:ZERO], T["%sp%d" % (name, t)][:, 0:ZERO], T.sd[:, 0:512]), after=0)
 
     V(lambda: vec.memset(T.sd[:, 0:512], 0.0))
     vec.wait_ge(S.iot, 2)
-    V(lambda: vec.tensor_scalar(T.ip[:, 1:2], T.ip[:, 0:1], 15, None, A.bitwise_and))
-    V(lambda: vec.tensor_scalar(T.ip[:, 2:3], T.ip[:, 1:2], 2, None, A.logical_shift_right))
-    V(lambda: vec.tensor_scalar(T.ip[:, 3:4], T.ip[:, 0:1], 3, None, A.bitwise_and))
-    V(lambda: vec.tensor_scalar(T.ip[:, 4:5], T.ip[:, 0:1], 4, None, A.logical_shift_right))
+    V(lambda: vec.tensor_scalar(T.ip[:, 1:2], T.ip[:, 0:1], 15, None, A.bitwise_and), after=0)
+    V(lambda: vec.tensor_scalar(T.ip[:, 2:3], T.ip[:, 0:1], 2, 3, A.logical_shift_right, A.bitwise_and), after=0)
+    V(lambda: vec.tensor_scalar(T.ip[:, 3:4], T.ip[:, 0:1], 3, None, A.bitwise_and), after=0)
+    V(lambda: vec.tensor_scalar(T.ip[:, 4:5], T.ip[:, 0:1], 4, None, A.logical_shift_right), after=0)
     V(lambda: vec.tensor_copy(T.cf[:, 0:4], T.ip[:, 1:5]))
     fb, fq, fr, fg = cf(0), cf(1), cf(2), cf(3)
-    b128, b64, base, bnum = cf(4), cf(5), cf(6), cf(7)
-    V(lambda: vec.tensor_scalar(b128, fb, 128.0, None, A.add))
+    b128, base, bnum = cf(4), cf(6), cf(7)
+    V(lambda: vec.tensor_scalar(b128, fb, float(ZERO), None, A.add))
     V(lambda: vec.tensor_scalar(T.cl[:], T.q32[:], fq, b128, A.is_equal, A.mult))
-    V(lambda: vec.memset(T.d1[:], -1.0))
     for u in range(1, R + 1):
         if (u - 1) % 2 == ab:
-            V(lambda: vec.tensor_scalar(cf(8 + u), fg, float(u - 1), None, A.is_equal))
+            V(lambda: vec.tensor_scalar(cf(8 + u), fg, float(u - 1), None, A.is_equal), after=0)
     if ab == 0:
-        zeros(1)
+        zeros("m", 1)
     vec.wait_ge(S.ld_s, 16)
-    d0_done = V(lambda: vec.quantize_mx(T.dq0[:, 0:144], T.dp0[:, 0:144], T.sd[:, 0:576]))
+    d0_done = V(lambda: vec.quantize_mx(T.dq0[:, 0:144], T.dp0[:, 0:144], T.sd[:, 0:576]), after=0)
 
-    def windows(t, sready=None):
-        q0, p0, wc, ws = T["dq%d" % (t - 1)], T["dp%d" % (t - 1)], T["wc%d" % t], T["ws%d" % t]
+    def windows(t, q0, p0, lst, ready=None):
+        wc, ws = T["wc%d" % t], T["ws%d" % t]
         for q in range(4):
-            vec.tensor_copy(u32(wc[:, 128 * q:128 * q + 128]), u32(q0[:, 0:144]).indirect(T.cl[:, 8 * q:8 * q + 8])).then_inc(S["wc%d" % q], 1)
-            if q < 3:
-                act(ws[:, 128 * q:128 * q + 128], p0[:, 0:144].indirect(T.cl[:, 8 * q:8 * q + 8]), CP).then_inc(S["ws%d" % q], 1)
-        if sready:
-            vec.wait_ge(sready[0], sready[1])
-        vec.tensor_copy(ws[:, 384:512], p0[:, 0:144].indirect(T.cl[:, 24:32])).then_inc(S.ws3, 1)
+            a, b, c, d = 128 * q, 128 * q + 128, 8 * q, 8 * q + 8
+            vec.tensor_copy(u32(wc[:, a:b]), u32(q0).indirect(lst[:, c:d])).then_inc(S["wc%d" % q], 1)
+            if q < 3 or not ready:
+                act(ws[:, a:b], p0.indirect(lst[:, c:d]), CP).then_inc(S["ws%d" % q], 1)
+            else:
+                vec.wait_ge(*ready)
+                vec.tensor_copy(ws[:, a:b], p0.indirect(lst[:, c:d])).then_inc(S["ws%d" % q], 1)
 
     vec.wait_ge(S.v, d0_done)
     cnt["vw"] = cnt["v"]
     g.scalar.wait_ge(S.v, d0_done)
-    windows(1)
+    windows(1, T.dq0[:, 0:144], T.dp0[:, 0:144], T.cl)
 
     g.scalar.wait_ge(S.iou, 3)
     AC(lambda: act(base, fq, ID, bias=float(HEAD), scale=256.0))
     AC(lambda: act(bnum, fq, ID, bias=float(P * rank), scale=256.0))
-    AC(lambda: act(b64, fb, ID, bias=64.0))
-    AC(lambda: act(T.ja[:], T.j4[:], ACT.Abs, bias=fr, scale=-1.0))
-    consts = AC(lambda: act(T.mk0[:], T.ja[:], ID, bias=-FAR, scale=2 * FAR))
+    sj = AC(lambda: act(T.ja[:], T.j4[:], ACT.Abs, bias=fr, scale=-1.0))
+    consts = AC(lambda: act(T.mk0[:], T.ja[:], ID, bias=-FAR, scale=2 * FAR), after=sj)
 
     def quant_x(k, a, n):
         return V(lambda: vec.quantize_mx(T["xq%d" % k][:, HEAD + a:HEAD + a + n], T["xp%d" % k][:, HEAD + a:HEAD + a + n],
-                                         T.xb[:, 4 * a:4 * (a + n)]))
+                                         T.xb[:, 4 * a:4 * (a + n)]), after=0)
 
     xdone = []
     for k in range(5):
@@ -238,7 +239,7 @@ def rank_program(g, core, T, topo):
                                    T.xq0[:, a:a + 256], T.xp0[:, a:a + 256], q == 0, q == 3)
         i.then_inc(S.t, 1)
 
-    ydone, wdone = {}, [0]
+    ydone, wdone, picked = {}, [0], {}
 
     def products(t):
         k = 2 * ((t - 1) % 3)
@@ -246,6 +247,9 @@ def rank_program(g, core, T, topo):
             g.tensor.wait_ge(S.v, wdone[0])
         if t == 4:
             g.tensor.wait_ge(S.s, ydone[1])
+        if t in picked:
+            g.tensor.wait_ge(S.v, picked[t][0])
+            g.tensor.wait_ge(S.s, picked[t][1])
         for o in range(O):
             g.tensor.matmul_mx(T["py%d" % (k + o)][:, 0:128], T.wq[:, 128 * o:128 * o + 128], T.wp[:, 128 * o:128 * o + 128],
                                T["dq%d" % t][:, 16:144], T["dp%d" % t][:, 16:144], True, True).then_inc(S.ty, 1)
@@ -257,7 +261,7 @@ def rank_program(g, core, T, topo):
         for o in range(O):
             out, in_ = T.ysb[:, 64 * o + 16 * (t - 1):64 * o + 16 * t], T["py%d" % (k + o)][:, 112:128]
             if both and o == 1:
-                g.scalar.wait_ge(S.v, V(lambda: vec.tensor_copy(out, in_)))
+                g.scalar.wait_ge(S.v, V(lambda: vec.tensor_copy(out, in_), after=0))
             else:
                 ydone[t] = AC(lambda: act(out, in_, CP))
 
@@ -288,20 +292,15 @@ def rank_program(g, core, T, topo):
             g.sync.dma_start(T.osc[4 * k:4 * k + 4, 16 * (t - 1):16 * t], dp[32 * k:32 * k + 4, 128:144]).then_inc(S.st, 16)
         cnt["st"] += 80
 
-    def send_numbers(t, num):
-        nl = T.nl[:, 8 * me:8 * me + 1]
-        g.wait_ge(S.v, V(lambda: vec.tensor_scalar(nl, num, cf(8 + t), num_acc[0], A.mult, A.add)))
-        to_peers(nl, nl, S.qn, 1)
-
-    def which_slot(t, i4):
+    def which_slot(t, ns):
         oh = tmp(4)
         if t == 1:
             d, dd = tmp(4), tmp(4)
-            V(lambda: vec.tensor_scalar(d, T.c8[:], i4, 0.5, A.subtract, A.add))
+            V(lambda: vec.tensor_scalar(d, T.c8[:], ns, 0.5, A.subtract, A.subtract), after=0)
             V(lambda: vec.tensor_tensor(dd, d, d, A.mult))
             V(lambda: vec.tensor_scalar(oh, dd, 1.0, cf(8 + t), A.is_lt, A.mult))
         else:
-            V(lambda: vec.tensor_scalar(oh, T.c4[:], i4, cf(8 + t), A.is_equal, A.mult))
+            V(lambda: vec.tensor_scalar(oh, T.c4[:], ns, cf(8 + t), A.is_equal, A.mult), after=0)
         if not oh_acc:
             oh_acc.append(oh)
         else:
@@ -309,22 +308,24 @@ def rank_program(g, core, T, topo):
             V(lambda: vec.tensor_tensor(oh2, oh, oh_acc[0], A.add))
             oh_acc[0] = oh2
 
-    def numbers(t, e, i4, ct):
-        own, fl, df, num = tmp(), tmp(), tmp(), tmp()
-        V(lambda: vec.tensor_scalar(own, ct, -1.0, bnum, A.mult, A.add))
+    def numbers(t, e, ns, ct):
+        own, fl, df, oo = tmp(), tmp(), tmp(), tmp()
+        vo = V(lambda: vec.tensor_scalar(own, ct, -1.0, bnum, A.mult, A.add), after=0)
         if t == 1:
-            V(lambda: vec.tensor_scalar(fl, i4, float(2 * me + 1 - N), None, A.is_equal))
+            V(lambda: vec.tensor_scalar(fl, ns, -float(2 * me + 1), cf(8 + t), A.is_equal, A.mult), after=0)
         else:
-            V(lambda: vec.tensor_scalar(fl, e, -1.0 / OUT, None, A.mult))
+            V(lambda: vec.tensor_scalar(fl, e, -1.0 / OUT, cf(8 + t), A.mult, A.mult), after=0)
         vec.wait_ge(S["yn%d" % t], MATE_INC)
-        V(lambda: vec.tensor_tensor(df, T["yn%d" % t][:, 0:1], own, A.subtract))
-        V(lambda: vec.tensor_scalar(num, df, fl, own, A.mult, A.add))
+        V(lambda: vec.tensor_tensor(df, T["yn%d" % t][:, 0:1], own, A.subtract), after=vo)
         if not num_acc:
             num_acc.append(tmp())
-            V(lambda: vec.tensor_scalar(num_acc[0], num, cf(8 + t), None, A.mult))
+            V(lambda: vec.tensor_scalar(oo, own, cf(8 + t), None, A.mult), after=vo)
+            V(lambda: vec.tensor_scalar(num_acc[0], df, fl, oo, A.mult, A.add))
         else:
-            send_numbers(t, num)
-        which_slot(t, i4)
+            nl = T.nl[:, 8 * me:8 * me + 1]
+            V(lambda: vec.tensor_scalar(oo, own, cf(8 + t), num_acc[0], A.mult, A.add), after=vo)
+            g.wait_ge(S.v, V(lambda: vec.tensor_scalar(nl, df, fl, oo, A.mult, A.add)))
+            to_peers(nl, nl, S.qn, 1)
 
     later = []
     for t in range(1, R + 1):
@@ -337,11 +338,11 @@ def rank_program(g, core, T, topo):
         mq, mp = T["mq" + n], T["mp" + n]
         score(t)
         vec.wait_ge(S.t, t)
-        V(lambda: vec.tensor_tensor(mk[:], T["mk%d" % (t - 1)][:], T.ps[:, 0:256], A.max))
+        V(lambda: vec.tensor_tensor(mk[:], T["mk%d" % (t - 1)][:], T.ps[:, 0:256], A.max), after=0)
         vr = V(lambda: vec.tensor_tensor_scan(rn[:], mk[:], mk[:], FAR, A.min, A.min))
         low = rn[:, 255:256]
         g.scalar.wait_ge(S.v, vr)
-        sct = AC(lambda: act(T.sg[:], rn[:], ACT.Sign, bias=low, scale=-1.0, accum_out=ct))
+        sct = AC(lambda: act(T.sg[:, 256 * t:256 * t + 256], rn[:], ACT.Sign, bias=low, scale=-1.0, accum_out=ct))
         off = T.ofs[:, 4 * t:4 * t + 1]
         sq, sp = T["xq%d" % source[t]], T["xp%d" % source[t]]
         e = None
@@ -349,7 +350,7 @@ def rank_program(g, core, T, topo):
             e, eb = tmp(), tmp()
             ym, low2 = T["ym" + n][:, 0:1], qm[:, 4 * slot:4 * slot + 1]
             vec.wait_ge(S["ym" + n], MATE_INC)
-            ve = V(lambda: vec.tensor_scalar(e, ym, low, -OUT, A.is_lt if ab == 0 else A.is_le, A.mult))
+            ve = V(lambda: vec.tensor_scalar(e, ym, low, -OUT, A.is_lt if ab == 0 else A.is_le, A.mult), after=vr)
             vm = V(lambda: vec.tensor_tensor(low2, ym, low, A.min), after=vr)
             vb = V(lambda: vec.tensor_scalar(eb, e, base, None, A.add), after=ve)
             g.wait_ge(S.v, vm)
@@ -362,16 +363,17 @@ def rank_program(g, core, T, topo):
             if flat:
                 to_roots(qm[:, 4 * slot:4 * slot + 1], low, S["qm" + n], 0)
                 if root:
-                    AC(lambda: act(qm[:, 4 * slot:4 * slot + 1], low, CP))
+                    scp = AC(lambda: act(qm[:, 4 * slot:4 * slot + 1], low, CP))
             else:
                 to_mate(T["ym" + n][:, 0:1], low, S["ym" + n])
             vec.wait_ge(S.s, sct)
-            vo = V(lambda: vec.tensor_scalar(off, ct, -1.0, base, A.mult, A.add))
+            vo = V(lambda: vec.tensor_scalar(off, ct, -1.0, base, A.mult, A.add), after=vr)
         if flat or root:
-            oq, op = mq[:, 16 * slot:16 * slot + 16], mp[:, 16 * slot:16 * slot + 16]
+            a = ZERO + 16 * slot
+            oq, op = mq[:, a:a + 16], mp[:, a:a + 16]
         else:
             oq, op = T["pq" + n][:, 0:16], T["pp" + n][:, 0:16]
-        vp = V(lambda: vec.tensor_copy(u32(oq), u32(sq[:, 0:HEAD + P]).indirect(off)))
+        vp = V(lambda: vec.tensor_copy(u32(oq), u32(sq[:, 0:HEAD + P]).indirect(off)), after=vo)
         g.scalar.wait_ge(S.v, vo)
         if merge:
             g.scalar.wait_ge(S["ys" + n], MATE_INC)
@@ -391,77 +393,83 @@ def rank_program(g, core, T, topo):
             to_mate(T["xp" + n][:, 0:16], op, S["ys" + n])
         if not root:
             yo = T["yo" + n][:, 0:1]
-            g.wait_ge(S.v, V(lambda: vec.tensor_scalar(yo, ct, -1.0, bnum, A.mult, A.add)))
+            g.wait_ge(S.v, V(lambda: vec.tensor_scalar(yo, ct, -1.0, bnum, A.mult, A.add), after=0))
             to_mate(T["yn" + n][:, 0:1], yo, S["yn" + n])
             if t < 3:
-                for u in range(1 if ab == 1 else 2, R + 1):
-                    zd = zeros(u)
+                for u in range(1, R + 1):
+                    zeros("d", u)
+                zd = zeros("m", t + 1)
                 g.scalar.wait_ge(S.v, zd)
             if t < R:
                 for c in cols:
                     quant_x(source[t + 1], *c)
             if t < 3:
                 vec.wait_ge(S.ld_w, 16)
-                wdone[0] = V(lambda: vec.quantize_mx(T.wq[:, 0:128 * O], T.wp[:, 0:128 * O], T.wb[:, 0:512 * O]))
+                wdone[0] = V(lambda: vec.quantize_mx(T.wq[:, 0:128 * O], T.wp[:, 0:128 * O], T.wb[:, 0:512 * O]), after=0)
             for f in later:
                 f()
             later = []
-        if t > 1:
-            products(t - 1)
-        if t == R and not root:
-            g.sync.wait_ge(S.v, resolve())
-            rows(T.res, ab)
+            if t > 1:
+                products(t - 1)
+            if t == R:
+                g.sync.wait_ge(S.v, resolve())
+                rows(T.res, ab)
+            vec.wait_ge(S.v, cnt["v"])
+            cnt["vw"] = cnt["v"]
         dq, dp = T["dq" + n], T["dp" + n]
         es = last_es if t == R else EM
         if root:
-            rm, d4, s4 = tmp(), tmp(nslot), tmp(nslot)
-            i4 = T.tmp[:, tcol[0] - 1:tcol[0]]
             if t == R:
-                own, fl, df, num = tmp(), tmp(), tmp(), tmp()
-                vown = V(lambda: vec.tensor_scalar(own, ct, -1.0, bnum, A.mult, A.add), after=vo)
-                V(lambda: vec.tensor_scalar(fl, e, -1.0 / OUT, None, A.mult), after=vo)
-                vec.wait_ge(S["yn" + n], MATE_INC)
-                V(lambda: vec.tensor_tensor(df, T["yn" + n][:, 0:1], own, A.subtract), after=vown)
-                V(lambda: vec.tensor_scalar(num, df, fl, own, A.mult, A.add))
-                send_numbers(t, num)
+                numbers(t, e, None, ct)
+            b = tcol[0] + nslot - 1
+            rm, rl = tmp(nslot), T.tmp[:, b:b + 1]
+            ns, o2f = T.ns[:, t:t + 1], tmp()
             inc = FLAT_INC if flat else PEER_INC
             vec.wait_ge(S["qm" + n], inc)
             if flat:
-                vec.wait_ge(S.s, own_s)
-            V(lambda: vec.tensor_reduce(rm, qm[:, 0:4 * nslot:4], X, A.min))
-            V(lambda: vec.tensor_scalar(d4, qm[:, 0:4 * nslot:4], rm, BIG, A.is_gt, A.mult))
-            V(lambda: vec.tensor_tensor_scan(s4, d4, T.d1[:, 0:nslot], BIG, A.min, A.add))
-            off2 = T.ofs[:, 4 * t + 2:4 * t + 3]
-            vo = V(lambda: vec.tensor_scalar(off2, i4, 16.0, b128 if flat else b64, A.mult, A.add))
+                vec.wait_ge(S.s, scp)
+            v = V(lambda: vec.tensor_tensor_scan(rm, qm[:, 0:4 * nslot:4], qm[:, 0:4 * nslot:4], FAR, A.min, A.min), after=vo)
+            g.scalar.wait_ge(S.v, v)
+            sns = AC(lambda: act(T.sh[:, 8 * t:8 * t + nslot], rm, ACT.Sign, bias=rl, scale=-1.0, accum_out=ns))
+            vec.wait_ge(S.s, sns)
+            off2, lst = T.ofs[:, 4 * t + 2:4 * t + 3], T["cm" + n]
+            vo = V(lambda: vec.tensor_scalar(off2, ns, -16.0, b128, A.mult, A.add), after=0)
+            vl = vo
+            if t < R:
+                vf = V(lambda: vec.tensor_scalar(o2f, ns, -16.0, b128, A.mult, A.add), after=0)
+                if not flat:
+                    vl = V(lambda: vec.tensor_scalar(lst[:], T.q32[:], fq, o2f, A.is_equal, A.mult), after=vf)
+            if t > 1:
+                products(t - 1)
             vec.wait_ge(S["qc" + n], inc)
             g.scalar.wait_ge(S["qs" + n], inc)
-            vp = V(lambda: vec.tensor_copy(u32(dq[:, 128:144]), u32(mq[:, 0:16 * nslot]).indirect(off2)))
+            wid = ZERO + 16 * nslot
+            vp = V(lambda: vec.tensor_copy(u32(dq[:, 128:144]), u32(mq[:, 0:wid]).indirect(off2)), after=vo)
+            if flat:
+                vl = V(lambda: vec.tensor_scalar(lst[:], T.q32[:], fq, o2f, A.is_equal, A.mult), after=vf)
             g.scalar.wait_ge(S.v, vo)
-            sp_ = AC(lambda: act(dp[:, 128:144], mp[:, 0:16 * nslot].indirect(off2), CP))
+            sp_ = AC(lambda: act(dp[:, 128:144], mp[:, 0:wid].indirect(off2), CP), after=sns)
+            picked[t] = (vp, sp_)
             g.wait_ge(S.v, vp)
             to_mate(u8(dq[:, 128:144]), u8(dq[:, 128:144]), S["dc" + n], es)
             g.wait_ge(S.s, sp_)
             to_mate(dp[:, 128:144], dp[:, 128:144], S["ds" + n])
             if t < R:
-                vec.wait_ge(S.v, vp)
-                cnt["vw"] = cnt["v"]
-                g.scalar.wait_ge(S.s, sp_)
-                cnt["sw"] = cnt["s"]
-                windows(t + 1, (S.s, sp_))
-                later.append(lambda t=t, e=e, i4=i4, ct=ct: numbers(t, e, i4, ct))
+                vec.wait_ge(S.v, vl)
+                cnt["vw"] = max(cnt["vw"], vl)
+                g.scalar.wait_ge(S.v, vl)
+                windows(t + 1, mq[:, 0:wid], mp[:, 0:wid], lst, (S["qs" + n], inc))
+                later.append(lambda t=t, e=e, ns=ns, ct=ct: (numbers(t, e, ns, ct), which_slot(t, ns)))
                 g.sync.wait_ge(S.t, t + 1)
-            else:
-                g.tensor.wait_ge(S.v, vp)
-                g.tensor.wait_ge(S.s, sp_)
             store(t, (S.v, vp), (S.s, sp_))
             if t == R:
                 products(R)
-                which_slot(t, i4)
+                which_slot(t, ns)
         else:
             if t < R:
                 vec.wait_ge(S["dc" + n], len(es))
                 g.scalar.wait_ge(S["ds" + n], MATE_INC)
-                windows(t + 1, (S["ds" + n], MATE_INC))
+                windows(t + 1, dq[:, 0:144], dp[:, 0:144], T.cl, (S["ds" + n], MATE_INC))
             else:
                 g.tensor.wait_ge(S["dc" + n], len(es))
                 g.tensor.wait_ge(S["ds" + n], MATE_INC)

from concourse.bass import DstId, RemoteDMATransfer
from concourse.mybir import dt, AluOpType, AxisListType, ActivationFunctionType

R, P, O, N = 4, 1024, 2, 8
HEAD = 64
ZERO = 128
F8 = "float8_e4m3fn_x4"
SCRATCH = {
    "xb": ("sbuf", [128, 4 * P], "bfloat16"),
    "wb": ("sbuf", [128, 512 * O], "bfloat16"),
    "sd": ("sbuf", [128, 576], "bfloat16"),
    "wq": ("sbuf", [128, 128 * O], F8), "wp": ("sbuf", [128, 128 * O], "uint8"),
    "ip": ("sbuf", [128, 8], "int32"),
    "q32": ("sbuf", [128, 32], "float32"),
    "j4": ("sbuf", [128, 256], "float32"),
    "ja": ("sbuf", [128, 256], "float32"),
    "c4": ("sbuf", [128, 4], "float32"),
    "c8": ("sbuf", [128, 4], "float32"),
    "cf": ("sbuf", [128, 16], "float32"),
    "cl": ("sbuf", [128, 32], "uint16"),
    "sg": ("sbuf", [128, 256 * (R + 1)], "bfloat16"),
    "sh": ("sbuf", [128, 8 * (R + 1)], "bfloat16"),
    "ct": ("sbuf", [128, 8], "float32"),
    "ns": ("sbuf", [128, 8], "float32"),
    "tmp": ("sbuf", [128, 256], "float32"),
    "ofs": ("sbuf", [128, 32], "uint16"),
    "nl": ("sbuf", [128, 32], "uint16"),
    "res": ("sbuf", [128, 4], "float32"),
    "resl": ("sbuf", [128, 4], "float32"),
    "ysb": ("sbuf", [128, 64 * O], "float32"),
    "ps": ("psum", [128, 512], "float32"),
}
for _t in range(R + 1):
    SCRATCH["xq%d" % _t] = ("sbuf", [128, HEAD + P], F8)
    SCRATCH["xp%d" % _t] = ("sbuf", [128, HEAD + P], "uint8")
    SCRATCH["dq%d" % _t] = ("sbuf", [128, ZERO + 16], F8)
    SCRATCH["dp%d" % _t] = ("sbuf", [128, ZERO + 16], "uint8")
    SCRATCH["mk%d" % _t] = ("sbuf", [128, 256], "float32")
    if _t:
        _m = N if _t == 1 else N // 2
        SCRATCH["rn%d" % _t] = ("sbuf", [128, 256], "float32")
        SCRATCH["cm%d" % _t] = ("sbuf", [128, 32], "uint16")
        SCRATCH["wc%d" % _t] = ("sbuf", [128, 512], F8)
        SCRATCH["ws%d" % _t] = ("sbuf", [128, 512], "uint8")
        SCRATCH["pq%d" % _t] = ("sbuf", [128, 16], F8)
        SCRATCH["pp%d" % _t] = ("sbuf", [128, 16], "uint8")
        SCRATCH["mq%d" % _t] = ("sbuf", [128, ZERO + 16 * _m], F8)
        SCRATCH["mp%d" % _t] = ("sbuf", [128, ZERO + 16 * _m], "uint8")
        SCRATCH["qm%d" % _t] = ("sbuf", [128, 4 * _m], "float32")
        SCRATCH["yo%d" % _t] = ("sbuf", [128, 4], "float32")
        SCRATCH["ym%d" % _t] = ("sbuf", [128, 4], "float32")
        SCRATCH["yn%d" % _t] = ("sbuf", [128, 4], "float32")
for _k in range(6):
    SCRATCH["py%d" % _k] = ("psum", [128, 512], "float32")
SEMAPHORES = ["v", "s", "t", "ty", "iot", "iou", "ls", "ld_s", "ld_w", "st", "sty", "qn", "rs"]
SEMAPHORES += ["ld%d" % q for q in range(5)] + ["wc%d" % q for q in range(4)] + ["ws%d" % q for q in range(4)]
SEMAPHORES += [n + "%d" % t for t in range(1, R + 1) for n in ("ym", "yn", "yc", "ys", "qm", "qc", "qs", "dc", "ds")]

FAR = 1e29
OUT = 8192.0


def rank_program(g, core, T, topo):
    rank = T.rank_of(core)
    if rank is None:
        return
    A = AluOpType
    X = AxisListType.X
    ACT = ActivationFunctionType
    CP, ID = ACT.Copy, ACT.Identity
    S = T.sem
    chips, ranks_of = [], {}
    for c in T.cores:
        if topo.chip(c) not in ranks_of:
            chips.append(topo.chip(c))
            ranks_of[topo.chip(c)] = []
        ranks_of[topo.chip(c)].append(c)
    me = chips.index(topo.chip(core))
    ab = ranks_of[chips[me]].index(core)
    mate = ranks_of[chips[me]][1 - ab]
    nch = len(chips)
    others = [chips[(me + k) % nch] for k in range(1, nch)]
    peers = [ranks_of[h][ab] for h in others]

    cnt = {"v": 0, "vw": 0, "s": 0, "sw": 0, "ty": 0, "ls": 0, "st": 0}

    def V(call, after=None):
        need = cnt["v"] if after is None else after
        if cnt["vw"] < need:
            g.vector.wait_ge(S.v, need)
            cnt["vw"] = need
        call().then_inc(S.v, 1)
        cnt["v"] += 1
        return cnt["v"]

    def AC(call, after=0):
        if cnt["sw"] < after:
            g.scalar.wait_ge(S.s, after)
            cnt["sw"] = after
        call().then_inc(S.s, 1)
        cnt["s"] += 1
        return cnt["s"]

    def bits(es):
        return sum(1 << e for e in es)

    def dst(c):
        a = topo.addr(c)
        return DstId(rid=a[0], pnc=a[1])

    ES = topo.engines(core, peers[0])[:8]
    EM = topo.engines(core, mate)[:16]
    EO = [e for e in EM if e not in ES][:8]
    MATE_INC = len(EM)
    PEER_INC = 8
    FLAT_INC = 16 + len(EO)
    last_es = EO

    def to_mate(out, in_, sem, es=None):
        es = EM if es is None else es
        rid, pid = topo.addr(mate)[:2]
        g.remote_dma(out, in_, sem, S.ls, pid, rid, bits(es))
        cnt["ls"] += len(es)

    def fused(parts):
        g.remote_dma_fused([RemoteDMATransfer(dst_ids=[dst(c)], dma_engine_mask=bits(e), remote_sem=sem, src=in_, dst=out)
                            for c, e, out, in_, sem in parts], local_sem=S.ls)
        cnt["ls"] += sum(len(p[1]) for p in parts)

    def cuts(turn):
        return [ES[0:4], ES[4:6], ES[6:8]] if turn == 0 else [ES[4:8], ES[0:2], ES[2:4]]

    def to_peers(out, in_, sem, turn):
        fused([(c, e, out, in_, sem) for c, e in zip(peers, cuts(turn))])

    def to_roots(out, in_, sem, turn):
        roots = [ranks_of[h][0] for h in others]
        parts = [(c, e, out, in_, sem) for c, e in zip(roots, cuts(turn))]
        fused(parts if ab == 0 else parts + [(mate, EO, out, in_, sem)])

    def u8(ap):
        return ap.bitcast(dt.uint8)

    def u32(ap):
        return ap.bitcast(dt.uint32)

    tcol = [0]

    def tmp(n=1):
        a = tcol[0]
        tcol[0] += n
        return T.tmp[:, a:a + n]

    vec = g.vector
    act = g.scalar.activation
    cols = [(0, 256), (256, 256), (512, 256), (768, 128), (896, 128)]
    g.sync.dma_start(T.sd[:, 512:576], T.seed[:]).then_inc(S.ld_s, 16)
    for k in range(5):
        a, n = cols[k]
        queue = g.sync if k % 2 == 0 else g.scalar
        queue.dma_start(T.xb[:, 4 * a:4 * (a + n)], T.x[:, 4 * a:4 * (a + n)]).then_inc(S["ld%d" % k], 16)
    g.sync.wait_ge(S.ld3, 16)
    g.sync.wait_ge(S.ld4, 16)
    g.sync.dma_start(T.wb[:], T.w[:]).then_inc(S.ld_w, 16)

    g.iota(T.ip[:, 0:1], [[0, 1]], 0, 1).then_inc(S.iot, 1)
    g.iota(T.q32[:], [[1, 4], [0, 8]], 0, 0, allow_small_or_imprecise_dtypes=True).then_inc(S.iot, 1)
    g.iota(T.j4[:], [[1, 4], [0, 64]], 0, 0, allow_small_or_imprecise_dtypes=True).then_inc(S.iou, 1)
    g.iota(T.c4[:], [[-1, 4]], 0, 0, allow_small_or_imprecise_dtypes=True).then_inc(S.iou, 1)
    g.iota(T.c8[:], [[-2, 4]], 0, 0, allow_small_or_imprecise_dtypes=True).then_inc(S.iou, 1)

    def cf(k):
        return T.cf[:, k:k + 1]

    def zeros(name, t):
        return V(lambda: vec.quantize_mx(T["%sq%d" % (name, t)][:, 0:ZERO], T["%sp%d" % (name, t)][:, 0:ZERO], T.sd[:, 0:512]), after=0)

    V(lambda: vec.memset(T.sd[:, 0:512], 0.0))
    vec.wait_ge(S.iot, 2)
    V(lambda: vec.tensor_scalar(T.ip[:, 1:2], T.ip[:, 0:1], 15, None, A.bitwise_and), after=0)
    V(lambda: vec.tensor_scalar(T.ip[:, 2:3], T.ip[:, 0:1], 2, 3, A.logical_shift_right, A.bitwise_and), after=0)
    V(lambda: vec.tensor_scalar(T.ip[:, 3:4], T.ip[:, 0:1], 3, None, A.bitwise_and), after=0)
    V(lambda: vec.tensor_scalar(T.ip[:, 4:5], T.ip[:, 0:1], 4, None, A.logical_shift_right), after=0)
    V(lambda: vec.tensor_copy(T.cf[:, 0:4], T.ip[:, 1:5]))
    fb, fq, fr, fg = cf(0), cf(1), cf(2), cf(3)
    b128, base, bnum = cf(4), cf(6), cf(7)
    V(lambda: vec.tensor_scalar(b128, fb, float(ZERO), None, A.add))
    V(lambda: vec.tensor_scalar(T.cl[:], T.q32[:], fq, b128, A.is_equal, A.mult))
    for u in range(1, R + 1):
        if (u - 1) % 2 == ab:
            V(lambda: vec.tensor_scalar(cf(8 + u), fg, float(u - 1), None, A.is_equal), after=0)
    if ab == 0:
        zeros("m", 1)
    vec.wait_ge(S.ld_s, 16)
    d0_done = V(lambda: vec.quantize_mx(T.dq0[:, 0:144], T.dp0[:, 0:144], T.sd[:, 0:576]), after=0)

    def windows(t, q0, p0, lst, ready=None):
        wc, ws = T["wc%d" % t], T["ws%d" % t]
        for q in range(4):
            a, b, c, d = 128 * q, 128 * q + 128, 8 * q, 8 * q + 8
            vec.tensor_copy(u32(wc[:, a:b]), u32(q0).indirect(lst[:, c:d])).then_inc(S["wc%d" % q], 1)
            if q < 3 or not ready:
                act(ws[:, a:b], p0.indirect(lst[:, c:d]), CP).then_inc(S["ws%d" % q], 1)
            else:
                vec.wait_ge(*ready)
                vec.tensor_copy(ws[:, a:b], p0.indirect(lst[:, c:d])).then_inc(S["ws%d" % q], 1)

    vec.wait_ge(S.v, d0_done)
    cnt["vw"] = cnt["v"]
    g.scalar.wait_ge(S.v, d0_done)
    windows(1, T.dq0[:, 0:144], T.dp0[:, 0:144], T.cl)

    g.scalar.wait_ge(S.iou, 3)
    AC(lambda: act(base, fq, ID, bias=float(HEAD), scale=256.0))
    AC(lambda: act(bnum, fq, ID, bias=float(P * rank), scale=256.0))
    sj = AC(lambda: act(T.ja[:], T.j4[:], ACT.Abs, bias=fr, scale=-1.0))
    consts = AC(lambda: act(T.mk0[:], T.ja[:], ID, bias=-FAR, scale=2 * FAR), after=sj)

    def quant_x(k, a, n):
        return V(lambda: vec.quantize_mx(T["xq%d" % k][:, HEAD + a:HEAD + a + n], T["xp%d" % k][:, HEAD + a:HEAD + a + n],
                                         T.xb[:, 4 * a:4 * (a + n)]), after=0)

    xdone = []
    for k in range(5):
        vec.wait_ge(S["ld%d" % k], 16)
        xdone.append(quant_x(0, *cols[k]))
    xdone[3] = xdone[4]
    vec.wait_ge(S.s, consts)
    source = {1: 0, 2: 0, 3: 3, 4: 3} if ab == 0 else {1: 0, 2: 2, 3: 2, 4: 4}

    def score(t):
        for q in range(4):
            if t == 1:
                g.tensor.wait_ge(S.v, xdone[q])
            g.tensor.wait_ge(S["wc%d" % q], t)
            g.tensor.wait_ge(S["ws%d" % q], t)
            a = HEAD + 256 * q
            i = g.tensor.matmul_mx(T.ps[:, 0:256], T["wc%d" % t][:, 128 * q:128 * q + 128], T["ws%d" % t][:, 128 * q:128 * q + 128],
                                   T.xq0[:, a:a + 256], T.xp0[:, a:a + 256], q == 0, q == 3)
        i.then_inc(S.t, 1)

    ydone, wdone, picked = {}, [0], {}

    def products(t):
        k = 2 * ((t - 1) % 3)
        if t == 1:
            g.tensor.wait_ge(S.v, wdone[0])
        if t == 4:
            g.tensor.wait_ge(S.s, ydone[1])
        if t in picked:
            g.tensor.wait_ge(S.v, picked[t][0])
            g.tensor.wait_ge(S.s, picked[t][1])
        for o in range(O):
            g.tensor.matmul_mx(T["py%d" % (k + o)][:, 0:128], T.wq[:, 128 * o:128 * o + 128], T.wp[:, 128 * o:128 * o + 128],
                               T["dq%d" % t][:, 16:144], T["dp%d" % t][:, 16:144], True, True).then_inc(S.ty, 1)
            cnt["ty"] += 1
        g.scalar.wait_ge(S.ty, cnt["ty"])
        both = t == R and ab == 0
        if both:
            vec.wait_ge(S.ty, cnt["ty"])
        for o in range(O):
            out, in_ = T.ysb[:, 64 * o + 16 * (t - 1):64 * o + 16 * t], T["py%d" % (k + o)][:, 112:128]
            if both and o == 1:
                g.scalar.wait_ge(S.v, V(lambda: vec.tensor_copy(out, in_), after=0))
            else:
                ydone[t] = AC(lambda: act(out, in_, CP))

    oh_acc, num_acc = [], []

    def rows(buf, which):
        for k in range(R):
            if k % 2 == which:
                g.sync.dma_start(T.nb[k:k + 1, :], buf[16 * k:16 * k + 16, 0:1]).then_inc(S.st, 16)
                cnt["st"] += 16

    def resolve():
        pr, nf = tmp(4), tmp(4)
        vec.wait_ge(S.qn, PEER_INC)
        V(lambda: vec.tensor_copy(nf, T.nl[:, 0:32:8]))
        V(lambda: vec.tensor_tensor(pr, oh_acc[0], nf, A.mult))
        v = V(lambda: vec.tensor_reduce(T.res[:, 0:1], pr, X, A.add))
        g.wait_ge(S.v, v)
        to_mate(T.resl[:, 0:1], T.res[:, 0:1], S.rs)
        return v

    def store(t, codes, scales):
        dq, dp = T["dq%d" % t], T["dp%d" % t]
        g.sync.wait_ge(*codes)
        g.sync.dma_start(T.oc[:, 64 * (t - 1):64 * t], u8(dq[:, 128:144])).then_inc(S.st, 16)
        g.sync.wait_ge(*scales)
        for k in range(4):
            g.sync.dma_start(T.osc[4 * k:4 * k + 4, 16 * (t - 1):16 * t], dp[32 * k:32 * k + 4, 128:144]).then_inc(S.st, 16)
        cnt["st"] += 80

    def which_slot(t, ns):
        oh = tmp(4)
        if t == 1:
            d, dd = tmp(4), tmp(4)
            V(lambda: vec.tensor_scalar(d, T.c8[:], ns, 0.5, A.subtract, A.subtract), after=0)
            V(lambda: vec.tensor_tensor(dd, d, d, A.mult))
            V(lambda: vec.tensor_scalar(oh, dd, 1.0, cf(8 + t), A.is_lt, A.mult))
        else:
            V(lambda: vec.tensor_scalar(oh, T.c4[:], ns, cf(8 + t), A.is_equal, A.mult), after=0)
        if not oh_acc:
            oh_acc.append(oh)
        else:
            oh2 = tmp(4)
            V(lambda: vec.tensor_tensor(oh2, oh, oh_acc[0], A.add))
            oh_acc[0] = oh2

    def numbers(t, e, ns, ct):
        own, fl, df, oo = tmp(), tmp(), tmp(), tmp()
        vo = V(lambda: vec.tensor_scalar(own, ct, -1.0, bnum, A.mult, A.add), after=0)
        if t == 1:
            V(lambda: vec.tensor_scalar(fl, ns, -float(2 * me + 1), cf(8 + t), A.is_equal, A.mult), after=0)
        else:
            V(lambda: vec.tensor_scalar(fl, e, -1.0 / OUT, cf(8 + t), A.mult, A.mult), after=0)
        vec.wait_ge(S["yn%d" % t], MATE_INC)
        V(lambda: vec.tensor_tensor(df, T["yn%d" % t][:, 0:1], own, A.subtract), after=vo)
        if not num_acc:
            num_acc.append(tmp())
            V(lambda: vec.tensor_scalar(oo, own, cf(8 + t), None, A.mult), after=vo)
            V(lambda: vec.tensor_scalar(num_acc[0], df, fl, oo, A.mult, A.add))
        else:
            nl = T.nl[:, 8 * me:8 * me + 1]
            V(lambda: vec.tensor_scalar(oo, own, cf(8 + t), num_acc[0], A.mult, A.add), after=vo)
            g.wait_ge(S.v, V(lambda: vec.tensor_scalar(nl, df, fl, oo, A.mult, A.add)))
            to_peers(nl, nl, S.qn, 1)

    later = []
    for t in range(1, R + 1):
        root, flat = (t - 1) % 2 == ab, t == 1
        merge = root and not flat
        n = "%d" % t
        mk, qm, rn, ct = T["mk" + n], T["qm" + n], T["rn" + n], T.ct[:, t:t + 1]
        slot = rank if flat else me
        nslot = N if flat else nch
        mq, mp = T["mq" + n], T["mp" + n]
        score(t)
        vec.wait_ge(S.t, t)
        V(lambda: vec.tensor_tensor(mk[:], T["mk%d" % (t - 1)][:], T.ps[:, 0:256], A.max), after=0)
        vr = V(lambda: vec.tensor_tensor_scan(rn[:], mk[:], mk[:], FAR, A.min, A.min))
        low = rn[:, 255:256]
        g.scalar.wait_ge(S.v, vr)
        sct = AC(lambda: act(T.sg[:, 256 * t:256 * t + 256], rn[:], ACT.Sign, bias=low, scale=-1.0, accum_out=ct))
        off = T.ofs[:, 4 * t:4 * t + 1]
        sq, sp = T["xq%d" % source[t]], T["xp%d" % source[t]]
        e = None
        if merge:
            e, eb = tmp(), tmp()
            ym, low2 = T["ym" + n][:, 0:1], qm[:, 4 * slot:4 * slot + 1]
            vec.wait_ge(S["ym" + n], MATE_INC)
            ve = V(lambda: vec.tensor_scalar(e, ym, low, -OUT, A.is_lt if ab == 0 else A.is_le, A.mult), after=vr)
            vm = V(lambda: vec.tensor_tensor(low2, ym, low, A.min), after=vr)
            vb = V(lambda: vec.tensor_scalar(eb, e, base, None, A.add), after=ve)
            g.wait_ge(S.v, vm)
            to_peers(low2, low2, S["qm" + n], 0)
            vec.wait_ge(S.s, sct)
            vo = V(lambda: vec.tensor_scalar(off, eb, ct, fb, A.subtract, A.max), after=vb)
            vec.wait_ge(S["yc" + n], MATE_INC)
        else:
            g.wait_ge(S.v, vr)
            if flat:
                to_roots(qm[:, 4 * slot:4 * slot + 1], low, S["qm" + n], 0)
                if root:
                    scp = AC(lambda: act(qm[:, 4 * slot:4 * slot + 1], low, CP))
            else:
                to_mate(T["ym" + n][:, 0:1], low, S["ym" + n])
            vec.wait_ge(S.s, sct)
            vo = V(lambda: vec.tensor_scalar(off, ct, -1.0, base, A.mult, A.add), after=vr)
        if flat or root:
            a = ZERO + 16 * slot
            oq, op = mq[:, a:a + 16], mp[:, a:a + 16]
        else:
            oq, op = T["pq" + n][:, 0:16], T["pp" + n][:, 0:16]
        vp = V(lambda: vec.tensor_copy(u32(oq), u32(sq[:, 0:HEAD + P]).indirect(off)), after=vo)
        g.scalar.wait_ge(S.v, vo)
        if merge:
            g.scalar.wait_ge(S["ys" + n], MATE_INC)
        own_s = AC(lambda: act(op, sp[:, 0:HEAD + P].indirect(off), CP))
        g.wait_ge(S.v, vp)
        if flat:
            to_roots(u8(oq), u8(oq), S["qc" + n], 1)
            g.wait_ge(S.s, own_s)
            to_roots(op, op, S["qs" + n], 0)
        elif root:
            to_peers(u8(oq), u8(oq), S["qc" + n], 1)
            g.wait_ge(S.s, own_s)
            to_peers(op, op, S["qs" + n], 0)
        else:
            to_mate(u8(T["xq" + n][:, 0:16]), u8(oq), S["yc" + n])
            g.wait_ge(S.s, own_s)
            to_mate(T["xp" + n][:, 0:16], op, S["ys" + n])
        if not root:
            yo = T["yo" + n][:, 0:1]
            g.wait_ge(S.v, V(lambda: vec.tensor_scalar(yo, ct, -1.0, bnum, A.mult, A.add), after=0))
            to_mate(T["yn" + n][:, 0:1], yo, S["yn" + n])
            if t < 3:
                for u in range(1, R + 1):
                    zeros("d", u)
                zd = zeros("m", t + 1)
                g.scalar.wait_ge(S.v, zd)
            if t < R:
                for c in cols:
                    quant_x(source[t + 1], *c)
            if t < 3:
                vec.wait_ge(S.ld_w, 16)
                wdone[0] = V(lambda: vec.quantize_mx(T.wq[:, 0:128 * O], T.wp[:, 0:128 * O], T.wb[:, 0:512 * O]), after=0)
            for f in later:
                f()
            later = []
            if t > 1:
                products(t - 1)
            if t == R:
                g.sync.wait_ge(S.v, resolve())
                rows(T.res, ab)
            vec.wait_ge(S.v, cnt["v"])
            cnt["vw"] = cnt["v"]
        dq, dp = T["dq" + n], T["dp" + n]
        es = last_es if t == R else EM
        if root:
            if t == R:
                numbers(t, e, None, ct)
            b = tcol[0] + nslot - 1
            rm, rl = tmp(nslot), T.tmp[:, b:b + 1]
            ns, o2f = T.ns[:, t:t + 1], tmp()
            inc = FLAT_INC if flat else PEER_INC
            vec.wait_ge(S["qm" + n], inc)
            if flat:
                vec.wait_ge(S.s, scp)
            v = V(lambda: vec.tensor_tensor_scan(rm, qm[:, 0:4 * nslot:4], qm[:, 0:4 * nslot:4], FAR, A.min, A.min), after=vo)
            g.scalar.wait_ge(S.v, v)
            sns = AC(lambda: act(T.sh[:, 8 * t:8 * t + nslot], rm, ACT.Sign, bias=rl, scale=-1.0, accum_out=ns))
            vec.wait_ge(S.s, sns)
            off2, lst = T.ofs[:, 4 * t + 2:4 * t + 3], T["cm" + n]
            vo = V(lambda: vec.tensor_scalar(off2, ns, -16.0, b128, A.mult, A.add), after=0)
            vl = vo
            if t < R:
                vf = V(lambda: vec.tensor_scalar(o2f, ns, -16.0, b128, A.mult, A.add), after=0)
                if not flat:
                    vl = V(lambda: vec.tensor_scalar(lst[:], T.q32[:], fq, o2f, A.is_equal, A.mult), after=vf)
            if t > 1:
                products(t - 1)
            vec.wait_ge(S["qc" + n], inc)
            g.scalar.wait_ge(S["qs" + n], inc)
            wid = ZERO + 16 * nslot
            vp = V(lambda: vec.tensor_copy(u32(dq[:, 128:144]), u32(mq[:, 0:wid]).indirect(off2)), after=vo)
            if flat:
                vl = V(lambda: vec.tensor_scalar(lst[:], T.q32[:], fq, o2f, A.is_equal, A.mult), after=vf)
            g.scalar.wait_ge(S.v, vo)
            sp_ = AC(lambda: act(dp[:, 128:144], mp[:, 0:wid].indirect(off2), CP), after=sns)
            picked[t] = (vp, sp_)
            g.wait_ge(S.v, vp)
            to_mate(u8(dq[:, 128:144]), u8(dq[:, 128:144]), S["dc" + n], es)
            g.wait_ge(S.s, sp_)
            to_mate(dp[:, 128:144], dp[:, 128:144], S["ds" + n])
            if t < R:
                vec.wait_ge(S.v, vl)
                cnt["vw"] = max(cnt["vw"], vl)
                g.scalar.wait_ge(S.v, vl)
                windows(t + 1, mq[:, 0:wid], mp[:, 0:wid], lst, (S["qs" + n], inc))
                later.append(lambda t=t, e=e, ns=ns, ct=ct: (numbers(t, e, ns, ct), which_slot(t, ns)))
                g.sync.wait_ge(S.t, t + 1)
            store(t, (S.v, vp), (S.s, sp_))
            if t == R:
                products(R)
                which_slot(t, ns)
        else:
            if t < R:
                vec.wait_ge(S["dc" + n], len(es))
                g.scalar.wait_ge(S["ds" + n], MATE_INC)
                windows(t + 1, dq[:, 0:144], dp[:, 0:144], T.cl, (S["ds" + n], MATE_INC))
            else:
                g.tensor.wait_ge(S["dc" + n], len(es))
                g.tensor.wait_ge(S["ds" + n], MATE_INC)
            store(t, (S["dc" + n], len(es)), (S["ds" + n], MATE_INC))
            if t == R:
                products(R)
        if t == R:
            g.scalar.wait_ge(S.s, cnt["s"])
            g.scalar.dma_start(T.y[:], T.ysb[:]).then_inc(S.sty, 16)
            v = resolve() if root else 0
            g.sync.wait_ge(S.rs, MATE_INC)
            rows(T.resl, 1 - ab)
            if root:
                g.sync.wait_ge(S.v, v)
                rows(T.res, ab)
    g.sync.wait_ge(S.st, cnt["st"])
    g.scalar.wait_ge(S.sty, 16)
    g.wait_ge(S.ls, cnt["ls"])
    g.wait_ge(S.v, cnt["v"])
    g.wait_ge(S.s, cnt["s"])
